import numpy as np, ml_dtypes
CORES = [2,6,10,14,18,22,26,30]
N = 8
BF = ml_dtypes.bfloat16
L, S, ST, GENS, K = 192, 8, 3, 2, 48
GW, XW = S * L, 16 * L
def parts(rng):
    g = rng.integers(0, XW, (N, 8, 16, GW)); h = rng.integers(0, GW, (N, 8, 16, GW)); x = rng.integers(0, 256, (N, 8, 16, XW))
    return g, h, x, rng.integers(0, 256, (N, 8, 16, L)), rng.integers(800, 1151, (N, 8))
def pack(g, h, x, a, t):
    return {"gn": np.ascontiguousarray(g.reshape(N, 128, GW)).astype(np.int32), "nb": np.ascontiguousarray(h.reshape(N, 128, GW)).astype(np.int32),
            "x": x.reshape(N, 128, XW).astype(np.float32).astype(BF), "th": np.repeat(t, 16, axis=1).reshape(N, 128, 1).astype(np.int32), "a0": a.reshape(N, 128, L).astype(np.float32).astype(BF)}
def setup_inputs(rng):
    return pack(*parts(rng))
def uneven(rng, n):
    v = np.floor(256 * rng.random((N, 8, 16, n)) * np.exp2(-rng.integers(0, 8, (N, 8, 1, n)).astype(np.float64))).astype(np.int64)
    return np.where(rng.random((N, 8, 1, n)) < 0.5, 255 - v, v)
def setup_inputs_spread(rng):
    g = (XW * rng.random((N, 8, 16, GW)) ** 3).astype(np.int64); h = (GW * rng.random((N, 8, 16, GW)) ** 2).astype(np.int64)
    g[:, 1::2] = XW - 1 - g[:, 1::2]; h[:, :, ::2] = GW - 1 - h[:, :, ::2]
    t = np.argsort(rng.random((N, 8)), axis=1) * 510 + rng.integers(0, 510, (N, 8))
    return pack(g, h, uneven(rng, XW), uneven(rng, L), t)
def twoends(rng, n):
    return np.where(rng.random((N, 8, 1, n)) < 0.7, 255 * rng.integers(0, 2, (N, 8, 1, n)), 255 * rng.integers(0, 2, (N, 8, 16, n)))
def setup_inputs_ends(rng):
    g, h, x, a, t = parts(rng)
    g = np.where(rng.random(g.shape) < 0.8, (XW - 1) * rng.integers(0, 2, g.shape), g); h = np.where(rng.random(h.shape) < 0.8, (GW - 1) * rng.integers(0, 2, h.shape), h)
    x = twoends(rng, XW); a = twoends(rng, L); x[..., 0] = 0; x[..., XW - 1] = 255
    for q in range(N): t[q, :7] = rng.permutation(np.array([0, 0, 4080, 4080, 4080, 2294, 2294]))
    t[:, 7] = 0
    for i in (0, 1, L - 2, L - 1):
        g[:, 7, 0, S * i] = XW - 1; h[:, 7, :, S * i] = GW - 1; a[:, 7, :, i] = 0
    g[:, 7, :15, GW - 1] = XW - 1; g[:, 7, 15, GW - 1] = 0
    return pack(g, h, x, a, t)
def setup_inputs_corners(rng):
    g, h, x, a, t = parts(rng); o = rng.permutation(8); t[:, o[0]] = 0; t[:, o[1]] = 4080
    for q in range(N):
        w = rng.permutation(o[2:])
        h[q, w[0]] = np.arange(GW); h[q, w[1]] = (GW - 1) * rng.integers(0, 2, (16, GW)); h[q, w[2]] = np.roll(np.arange(GW), -1)
        g[q, w[3]] = (XW - 1) * rng.integers(0, 2, (16, GW))
        b = w[4]; t[q, b] = 0; x[q, b, :, XW - 1] = 255; g[q, b, 15] = XW - 1
        i = rng.permutation(L)[:L // 2]; a[q, b][:, i] = x[q, b][:, g[q, b, 0, S * i]]
        x[q, w[5]] = 255 * rng.integers(0, 2, (16, XW))
    return pack(g, h, x, a, t)
def setup_inputs_ties(rng):
    g, h, x, a, t = parts(rng)
    x = 8 * rng.integers(0, 32, (N, 8, 1, XW)) + ((np.arange(16)[:, None] == rng.integers(0, 16, (N, 8, 1, XW))) & (rng.random((N, 8, 1, XW)) < 0.5))
    a = 8 * rng.integers(0, 32, (N, 8, 1, L)) + np.zeros((16, 1), np.int64)
    h[:, ::2] = h[:, ::2, :1]
    return pack(g, h, x, a, 16 * (8 * rng.integers(0, 6, (N, 8)) + 1))
def setup_inputs_counts(rng):
    g, h, x, a, t = parts(rng); q = rng.permutation(N); o = rng.permutation(8); w = int(o[0])
    t[q[0]] = 0; t[q[1]] = 4080; t[q[2]] = 4080; t[q[2], o[1:4]] = 0; t[q[3]] = 0
    if N > 4: t[q[4]] = 1170
    if N > 5: t[q[5], o[1:5]] = 0
    t[:, w] = 0; t[q[1], w] = 4080
    u = np.floor(rng.integers(2, 7, (N, 1, XW)) * rng.random((N, 16, XW))).astype(np.int64); u[:, 0] = 0
    x[:, w] = u; x[q[1], w] = 255 - u[q[1]]; x[q[1], w, 0] = 254
    a[:, w] = 255; a[:, w, 0] = 254
    for r, n in ((q[2], 64), (q[3], 8 * int(rng.integers(3, 5)) + int(rng.choice(np.array([2, 3, 5, 6]))))):
        i = rng.permutation(L)[:n]; a[r, w, 0, i] = 255; h[r, w, 0, S * i] = S * i
    return pack(g, h, x, a, t)
def check_inputs(d):
    bad = []
    for k, lo, hi in (("gn", 0, XW - 1), ("nb", 0, GW - 1), ("x", 0, 255), ("th", 0, 4080), ("a0", 0, 255)):
        v = np.asarray(d[k]).astype(np.float64)
        if not (np.min(v) >= lo and np.max(v) <= hi): bad.append("range of " + k)
        elif np.any(v != np.floor(v)): bad.append("whole numbers of " + k)
    v = np.asarray(d["th"]).reshape(-1, 16)
    if np.any(v != v[:, :1]): bad.append("equal rows of th in a group")
    return bad
def reference(gn, nb, x, th, a0):
    G = gn.astype(np.int64).reshape(N, 8, 16, GW); H = nb.astype(np.int64).reshape(N, 8, 16, GW); X = x.astype(np.float32).astype(np.int64).reshape(N, 8, 16, XW)
    lim = th.astype(np.int64).reshape(N, 8, 16)[:, :, :1]; a = a0.astype(np.float32).astype(np.int64).reshape(N, 8, 16, L)
    A = np.zeros(N, np.int64); lane = np.arange(L); kk = np.arange(16)[None, :, None]
    for gen in range(GENS):
        h = np.zeros((N, 8, L), np.int64) + S * lane; p = np.zeros((N, 8, L), np.int64); err = np.zeros((N, 8, L), np.int64)
        dau = G[..., ::S].copy()
        for t in range(ST):
            now = np.zeros(N, np.int64)
            for r in range(N):
                q = (r + t) % N; hr = h[r][:, None, :]; pr = p[r]
                n = np.take_along_axis(np.take_along_axis(G[q], hr, 2), pr[:, None, :], 1)[:, 0]
                T = np.abs(np.take_along_axis(X[q], n[:, None, :], 2) - a[r])
                ho = np.take_along_axis(H[q], hr, 2)
                at = ((pr[:, None, :] + kk) & 15) * GW + ho
                e = np.take_along_axis(G[q].reshape(8, 16 * GW), at.reshape(8, 16 * L), 1)
                v = np.take_along_axis(X[q], e[:, None, :], 2).reshape(8, 16, 16, L)
                D = np.add.reduce(np.abs(v + T[:, :, None, :] - 255), axis=1)
                ok = D <= (lim[q] + (A[q] & 63))[:, :, None]
                found = np.any(ok, axis=1); m = np.argmax(ok, axis=1)
                em = np.take_along_axis(e.reshape(8, 16, L), m[:, None, :], 1)[:, 0]; hm = np.take_along_axis(ho, m[:, None, :], 1)[:, 0]
                an = np.where(found[:, None, :], np.take_along_axis(X[q], em[:, None, :], 2), T)
                dau[r, :, t] = np.where(found, em, n); h[r] = np.where(found, hm, h[r]); p[r] = (pr + 1 + np.where(found, m, 0)) & 15
                err[r] = err[r] + np.where(found, 0, 1); now[q] = np.sum(np.where(found, 0, 1)); a[r] = an
                np.put_along_axis(X[q], (16 * lane + p[r])[:, None, :], an, 2)
            A = now
        order = np.argsort(err * L + lane, axis=2)
        best = np.take_along_axis(dau, order[:, :, None, :K], 3)
        come = np.where((np.arange(K) & 1) == 1, np.roll(best, 1, axis=0), best)
        worst = order[:, :, ::-1][:, :, :K]
        np.put_along_axis(G, (S * worst)[:, :, None, :], come, 3)
    return {"yg": G[..., ::S].reshape(N, 128, L).astype(np.float32), "ya": a.reshape(N, 128, L).astype(np.float32), "ys": np.add.reduce(X.reshape(N, 8, 16, L, 16), axis=4).reshape(N, 128, L).astype(np.float32)}

@@ -1,0 +1,539 @@
+from concourse.bass import DstId, RemoteDMATransfer
+from concourse.mybir import AluOpType, ActivationFunctionType
+
+AL, AF = AluOpType, ActivationFunctionType
+NR, L, ST, GENS, KR = 8, 192, 3, 2, 48
+GW, XW = 1536, 3072
+C = 12
+EC, CW = 4, 48
+YC, YW, KG = 2, 96, 4
+VG = "SSSV"
+POOL = {"f32": ("float32", 11000), "bf": ("bfloat16", 28000), "hf": ("float16", 15000), "u16": ("uint16", 4600), "i32": ("int32", 3600)}
+SIZE = {"f32": 4, "bf": 2, "hf": 2, "u16": 2, "i32": 4}
+SCRATCH = {"p_" + k: ("sbuf", [128, v[1]], v[0]) for k, v in POOL.items()}
+SCRATCH.update({"bank%d" % b: ("psum", [128, 512], "float32") for b in range(8)})
+SEMAPHORES = ["sV", "sS", "sP", "sG", "left"] + ["d%d" % i for i in range(10)] + ["r%d" % i for i in range(40)]
+CY = 0.00083
+COST = {"f": 1.25, "gather": 1.56, "scatter": 3.5, "issue": 0.9, "hop": 2.2, "sem": 0.06, "pe": 0.00042}
+
+
+def rank_program(g, core, T, topo):
+    rank = T.rank_of(core)
+    if rank is None:
+        return
+    tasks, used, rings = [], {k: 0 for k in POOL}, {}
+    bank_use = [dict() for _ in range(8)]
+    ndma, nrem = [0], [0]
+
+    def mk(b, lo, n, mut=False, pre=()):
+        return {"b": b, "lo": lo, "n": n, "wr": [], "rd": [], "mut": mut, "pre": pre}
+
+    def tile(pool, n, mut=False):
+        lo, al = used[pool], 32 // SIZE[pool]
+        used[pool] = (lo + n + al - 1) // al * al
+        assert used[pool] <= POOL[pool][1]
+        return mk("p_" + pool, lo, n, mut)
+
+    def ring(pool, n, key):
+        if key not in rings:
+            rings[key] = tile(pool, n)
+        else:
+            o = rings[key]
+            rings[key] = mk(o["b"], o["lo"], n, False, [i for i, _ in o["wr"]] + o["rd"])
+        return rings[key]
+
+    def ps(bank):
+        t = mk("bank%d" % bank, 0, 512)
+        t["bank"] = bank
+        return t
+
+    def ap(t, a=0, b=None, st=1):
+        b = t["n"] if b is None else b
+        buf = T[t["b"]]
+        return buf[:, t["lo"] + a:t["lo"] + b] if st == 1 else buf[:, t["lo"] + a:t["lo"] + b:st]
+
+    def task(q, dur, ins, outs, fn, kind="c", extra=None, boost=0.0):
+        i, deps = len(tasks), {}
+        for t in ins:
+            for w, lag in t["wr"]:
+                deps[w] = max(deps.get(w, 0), lag)
+        for t in outs:
+            for w in t["pre"]:
+                deps.setdefault(w, 0)
+            if t["mut"]:
+                for w, lag in t["wr"]:
+                    deps[w] = max(deps.get(w, 0), lag)
+                for r in t["rd"]:
+                    deps.setdefault(r, 0)
+        for t in list(ins) + list(outs):
+            if "bank" in t:
+                bu = bank_use[t["bank"]]
+                for q2 in list(bu):
+                    if q2 != q:
+                        for j in bu[q2]:
+                            deps.setdefault(j, 0)
+                        bu[q2] = []
+                if i not in bu.setdefault(q, []):
+                    bu[q].append(i)
+        deps.pop(i, None)
+        tasks.append({"q": q, "dur": dur, "deps": deps, "fn": fn, "kind": kind, "x": extra, "soft": set(), "boost": boost})
+        for t in outs:
+            if t["mut"]:
+                t["wr"], t["rd"] = [], []
+            t["wr"].append((i, 0))
+        for t in ins:
+            t["rd"].append(i)
+        return i
+
+    def soft(i, j):
+        if j not in tasks[i]["deps"]:
+            tasks[i]["deps"][j] = 0
+            tasks[i]["soft"].add(j)
+
+    def vc(n, f=1.0):
+        return (0.05 + max(64, n * f) * CY) * COST["f"]
+
+    def gc_(n, k="gather"):
+        return (0.06 + n * COST[k] * CY) * COST["f"]
+
+    def ts(out, oa, in0, s1, op0, s2, op1, ins, n, f=1.0, boost=0.0):
+        def fn():
+            if op1 is None:
+                return [g.vector.tensor_scalar(oa, in0, s1, None, op0)]
+            return [g.vector.tensor_scalar(oa, in0, s1, s2, op0, op1)]
+        return task("V", vc(n, f), ins, [out], fn, boost=boost)
+
+    def tt(out, oa, in0, in1, op, ins, n=0, f=1.0, dur=None, boost=0.0):
+        return task("V", vc(n, f) if dur is None else dur, ins, [out], lambda: [g.vector.tensor_tensor(oa, in0, in1, op)], boost=boost)
+
+    def tcopy(out, oa, in0, ins, n=0, f=1.0, dur=None):
+        return task("V", vc(n, f) if dur is None else dur, ins, [out], lambda: [g.vector.tensor_copy(oa, in0)])
+
+    def act(out, oa, in0, func, ins, n=0, dur=None, bias=0.0, scale=1.0, acc=None, boost=0.0):
+        return task("S", vc(n) if dur is None else dur, ins, [out] + ([acc] if acc else []),
+                    lambda: [g.scalar.activation(oa, in0, func, bias=bias, scale=scale, accum_out=ap(acc) if acc else None)], boost=boost)
+
+    def iota(out, pat, base, cm, flag=True):
+        task("G", 0.13 + 2 * out["n"] * CY, [], [out], lambda: [g.iota(ap(out), pat, base, cm, allow_small_or_imprecise_dtypes=flag)])
+
+    def mms(out, ins, lst, f32=1, boost=0.0, after=None):
+        def fn():
+            r = []
+            for o, l, x, a, b, n in lst:
+                m = g.tensor.matmul(o, l, x, a, b)
+                if b:
+                    r.append(m)
+            return r or [m]
+        i = task("P", (0.03 + sum(max(64, m[5]) for m in lst) * COST["pe"] * f32) * COST["f"], ins, [out], fn, boost=boost)
+        if after:
+            for w, _ in after["wr"][:-1]:
+                soft(i, w)
+
+    def load(q, out, oa, src, dur):
+        e = g.sync if q == "Y" else g.scalar
+        i = task(q, 0.1, [], [out], lambda: [e.dma_start(oa, src)], "d", ndma[0])
+        out["wr"] = [(w, dur if w == i else lg) for w, lg in out["wr"]]
+        ndma[0] += 1
+
+    def store(dst, oa, ins):
+        task("Y", 0.1, ins, [], lambda: [g.sync.dma_start(dst, oa)], "d", ndma[0])
+        ndma[0] += 1
+
+    def engines(a, b):
+        return topo.engines(a, b)[:8]
+
+    def send(src, sa, moves, boost=0.0):
+        got, out, n = [], [], len(moves)
+        trs = []
+        for m, (dst, da, d) in enumerate(moves):
+            to, fr = T.cores[(rank + d) % NR], T.cores[(rank - d) % NR]
+            name = "r%d" % nrem[0]
+            nrem[0] += 1
+            rid, pid, _ = topo.addr(to)
+            es = engines(core, to)
+            es = es[m * len(es) // n:(m + 1) * len(es) // n]
+            trs.append((rid, pid, sum(1 << e for e in es), name, da))
+            got.append((name, len(engines(fr, core)) // n))
+            out.append(len(es))
+
+        def fn():
+            if n == 1:
+                rid, pid, mask, name, da = trs[0]
+                g.remote_dma(da, sa, T.sem[name], T.sem.left, pid, rid, mask)
+            else:
+                g.remote_dma_fused([RemoteDMATransfer(dst_ids=[DstId(rid=rid, pnc=pid)], dma_engine_mask=mask, remote_sem=T.sem[name], src=sa, dst=da)
+                                    for rid, pid, mask, name, da in trs], local_sem=T.sem.left)
+            return []
+        i = task("G", COST["issue"], [src], [], fn, "r", (got, sum(out)), boost)
+        for m, (dst, da, d) in enumerate(moves):
+            dst["wr"].append(((i, m), COST["hop"] + src["n"] * 512 / 60000.0))
+
+    gni, nbi, thi = tile("i32", GW), tile("i32", GW), tile("i32", 1)
+    XB = tile("bf", XW + L)
+    X, ext = mk(XB["b"], XB["lo"], XW, True), mk(XB["b"], XB["lo"] + XW, L, True)
+    a = tile("bf", L)
+    load("Y", thi, ap(thi), T.th[:], 3.0)
+    load("Y", gni, ap(gni), T.gn[:], 5.0)
+    load("S", nbi, ap(nbi), T.nb[:], 6.5)
+    load("S", X, ap(X), T.x[:], 8.0)
+    load("Y", a, ap(a), T.a0[:], 8.0)
+
+    def col(ins, src, s1, op0, s2=None, op1=None, n=1, pool="f32", f=1.0):
+        t = tile(pool, n)
+        ts(t, ap(t), src, s1, op0, s2, op1, ins, n, f)
+        return t
+
+    def acol(src, scale, bias):
+        t = tile("f32", src["n"])
+        act(t, ap(t), ap(src), AF.Identity, [src], src["n"], scale=scale, bias=bias)
+        return t
+    ip, ckr, ci = tile("i32", 1), tile("i32", 16), tile("i32", C)
+    im, kpat = tile("f32", 144), tile("bf", 16 * CW)
+    mgf, msf, ii0 = tile("f32", 128), tile("f32", 128), tile("f32", 12)
+    iota(ip, [[0, 1]], 0, 1, False)
+    iota(im, [[1, 144]], 0, 0)
+    iota(kpat, [[0, CW], [1, 16]], 0, 0)
+    iota(mgf, [[1, 8], [0, 16]], 0, 0)
+    iota(ii0, [[16, 12]], 0, 0)
+    iota(ckr, [[-1, 16]], 16, 1, False)
+    iota(ci, [[1, C]], 0, 0, False)
+    iota(msf, [[0, 8], [1, 16]], 0, 0)
+    si = col([ip], ap(ip), 15, AL.bitwise_and, pool="i32")
+    gi = col([ip], ap(ip), 4, AL.arith_shift_right, pool="i32")
+    scol = col([si], ap(si), 0.0, AL.add)
+    zc = col([gi], ap(gi), 16.0, AL.mult, 15.0, AL.add)
+    gcol = col([gi], ap(gi), 0.0, AL.add)
+    pcol = col([ip], ap(ip), 0.0, AL.add)
+    oh0 = col([scol], ap(scol), 0.0, AL.is_equal)
+    k16 = col([scol], ap(scol), 16.0, AL.add)
+    rm3 = col([scol], ap(scol), 3.0, AL.is_ge)
+    mask0 = col([kpat, scol], ap(kpat), ap(scol), AL.is_equal, n=16 * CW, pool="bf", f=0.5)
+    Zh = col([im, zc], ap(im), ap(zc), AL.is_equal, n=144, pool="hf")
+    Zb = col([im, zc], ap(im), ap(zc), AL.is_equal, n=144, pool="bf")
+    Zk = col([Zh, k16], ap(Zh), ap(k16), AL.mult, n=144, pool="hf", f=0.5)
+    Idb = col([im, pcol], ap(im, 0, 128), ap(pcol), AL.is_equal, n=128, pool="bf")
+    Blk = col([mgf, gcol], ap(mgf), ap(gcol), AL.is_equal, n=128, pool="bf")
+    lt = col([im, pcol], ap(im, 0, 128), ap(pcol), AL.is_gt, n=128, pool="bf")
+    Tri = tile("bf", 128)
+    tt(Tri, ap(Tri), ap(lt), ap(Blk), AL.mult, [lt, Blk], 128, 2)
+    RS = col([im, oh0], ap(im, 0, 128), 0.0, AL.mult, ap(oh0), AL.add, n=128)
+    Idh = col([im, pcol], ap(im, 0, 128), ap(pcol), AL.is_equal, n=128, pool="hf")
+    Lt = []
+    for t in range(ST):
+        eq = col([msf], ap(msf), float(t), AL.is_equal, n=128, pool="bf")
+        Lt.append(tile("hf", 128))
+        tt(Lt[t], ap(Lt[t]), ap(eq), ap(Blk), AL.mult, [eq, Blk], 128, 2)
+    cki = col([ckr], ap(ckr), 15, AL.bitwise_and, n=16, pool="i32")
+    ck = col([cki], ap(cki), 0.0, AL.add, n=16)
+    cidx = tile("u16", C)
+    tcopy(cidx, ap(cidx), ap(ci), [ci], C)
+    ii = col([ii0, scol], ap(ii0), ap(scol), AL.add, n=12)
+    hU0, I2, xi = acol(ii, 8.0, -1536.0), acol(ii, 1.0, 1536.0), acol(ii, 16.0, 0.0)
+    i48, i144, one = acol(ii, 1.0, 48.0), acol(ii, -1.0, 144.0), acol(ii, 0.0, 1.0)
+    ones = tile("bf", L)
+    act(ones, ap(ones), ap(kpat, 0, L), AF.Identity, [kpat], L, scale=0.0, bias=1.0)
+    thf = col([thi], ap(thi), 0.0, AL.add)
+    own_nb = ap(nbi, 0, GW, 8)
+    El0 = tile("u16", L)
+    tcopy(El0, ap(El0), own_nb, [nbi], L)
+    NBh0 = col([nbi], own_nb, -1536.0, AL.add, n=L)
+    G = tile("f32", GW, True)
+    ts(G, ap(G), ap(gni), -1536.0, AL.add, None, None, [gni], GW)
+    NBf = tile("f32", GW)
+    for j in range(4):
+        ts(NBf, ap(NBf, 384 * j, 384 * j + 384), ap(nbi, 384 * j, 384 * j + 384), -1536.0, AL.add, None, None, [nbi], 384)
+    own = tile("f32", 48 + L)
+    act(own, ap(own, 48, 48 + L), ap(G, 0, GW, 8), AF.Copy, [G], L)
+
+    def Z(z, k):
+        return ap(z, 15 - k, 143 - k)
+
+    lim = thf
+    for gen in range(GENS):
+        mo, mother = tile("hf", L), tile("hf", L)
+        ts(mo, ap(mo), ap(own, 48, 48 + L), ap(rm3), AL.mult, None, None, [own, rm3], L, boost=-30)
+        send(mo, ap(mo), [(mother, ap(mother), 2)], boost=-30)
+        hp = None
+        vs, fs = [], []
+        for t in range(ST):
+            last = t == ST - 1
+            nM = tile("hf", L)
+            if t == 0:
+                NBh, El, mask = NBh0, El0, mask0
+                inM = ts(nM, ap(nM), ap(G, 0, GW, 8), ap(oh0), AL.mult, None, None, [G, oh0], L)
+                hU, hUa, pw1 = hU0, ap(hU0), one
+            else:
+                PM = tile("bf", L)
+                tt(PM, ap(PM), ap(hp, 0, C).indirect(ap(cidx)), ap(mask0, 0, L), AL.mult, [hp, cidx, mask0], dur=gc_(L))
+                pr = ps(1)
+                mms(pr, [PM, Blk], [(ap(pr, 0, L), ap(Blk), ap(PM), True, True, L)])
+                prb = tile("bf", L)
+                act(prb, ap(prb), ap(pr, 0, L), AF.Copy, [pr], L)
+                hl = tile("u16", C)
+                ts(hl, ap(hl), ap(hp, C, 2 * C), 1536.0, AL.add, None, None, [hp], C, boost=50)
+                NBh, El = tile("f32", L), tile("u16", L)
+                act(NBh, ap(NBh), ap(NBf).indirect(ap(hl)), AF.Copy, [NBf, hl], dur=gc_(L), boost=50)
+                ts(El, ap(El), ap(NBh), 1536.0, AL.add, None, None, [NBh], L, boost=50)
+                mask = ring("bf", 16 * L, "mask")
+                for k in range(16):
+                    ts(mask, ap(mask, k, 16 * L, 16), ap(prb), ap(ck, k, k + 1), AL.is_equal, None, None, [prb, ck], L, 0.5)
+                inM = tt(nM, ap(nM), ap(G).indirect(ap(hl)), ap(mask, 0, 16 * L, 16), AL.mult, [G, hl, mask], dur=gc_(L))
+                hU, hUa, pw1 = hp, ap(hp, C, 2 * C), tile("f32", C)
+                act(pw1, ap(pw1), ap(hp, 0, C), AF.Identity, [hp], C, bias=1.0)
+            V, Vj, iG, iW = ring("bf", 16 * L, "V"), [], [], []
+            Wp = ps(0)
+            for j in range(EC):
+                Gg = ring("hf", 16 * CW, ("Gg", j))
+                m0 = 0 if t == 0 else 16 * CW * j
+                iG.append(tt(Gg, ap(Gg), ap(G).indirect(ap(El, j * CW, j * CW + CW)), ap(mask, m0, m0 + 16 * CW), AL.mult, [G, El, mask], dur=gc_(16 * CW)))
+                mms(Wp, [Gg, Zh], [(ap(Wp, j * CW, j * CW + CW), Z(Zh, k), ap(Gg, k, 16 * CW, 16), k == 0, k == 15, CW) for k in range(16)])
+                Wl = tile("u16", CW)
+                iW.append(ts(Wl, ap(Wl), ap(Wp, j * CW, j * CW + CW), 1536.0, AL.add, None, None, [Wp], CW, boost=50))
+                Vv = mk(V["b"], V["lo"] + 16 * CW * j, 16 * CW, False, V["pre"])
+                if VG[j] == "V":
+                    tcopy(Vv, ap(Vv), ap(X).indirect(ap(Wl)), [X, Wl], dur=gc_(16 * CW))
+                else:
+                    act(Vv, ap(Vv), ap(X).indirect(ap(Wl)), AF.Copy, [X, Wl], dur=gc_(16 * CW))
+                V["wr"] += Vv["wr"]
+                Vj.append(Vv)
+                if j == 0:
+                    npz = ps(1)
+                    mms(npz, [nM, Zh], [(ap(npz, 0, C), Z(Zh, r), ap(nM, r, L, 16), r == 0, r == 15, C) for r in range(16)])
+                    nl, df = tile("u16", C), tile("bf", L)
+                    inl = ts(nl, ap(nl), ap(npz, 0, C), 1536.0, AL.add, None, None, [npz], C, boost=50)
+                    idf = tt(df, ap(df), ap(X).indirect(ap(nl)), ap(a), AL.subtract, [X, nl, a], dur=gc_(L), boost=50)
+                    act(ext, ap(ext), ap(df), AF.Abs, [df], L, boost=50)
+            seq = [iG[0], inM, iW[0], iG[1], inl, iW[1], iG[2], idf, iW[2], iG[3], iW[3]]
+            for u, v in zip(seq, seq[1:]):
+                soft(v, u)
+            FI, Q, ok = tile("hf", L), tile("hf", 2 * L), tile("bf", L)
+            for y in range(YC):
+                i0, i1 = y * YW, y * YW + YW
+                vin = [Vj[j] for j in range(EC) if i0 <= j * CW < i1]
+                Dp = ps(2 + y)
+                D = ap(Dp, 0, YW)
+                Te = ap(ext, i0, i1)
+                for q in range(16 // KG):
+                    Y, lst, dl = ps(4 + (y * 4 + q) % 3), [], []
+                    ya = ring("bf", KG * YW, ("ya", y, q))
+                    for kk in range(KG):
+                        k = q * KG + kk
+                        o, v = ap(Y, kk * YW, kk * YW + YW), ap(V, 16 * i0 + k, 16 * i1, 16)
+                        lst += [(o, ap(Idb), v, True, False, YW), (o, ap(Idb), Te, False, True, YW)]
+                        dl.append((D, Z(Zb, k), ap(ya, kk * YW, kk * YW + YW), k == 0, k == 15, YW))
+                    mms(Y, vin + [Idb, ext], lst)
+                    act(ya, ap(ya), ap(Y, 0, KG * YW), AF.Abs, [Y], KG * YW, bias=-255.0)
+                    mms(Dp, [ya, Zb], dl, after=Dp, boost=20)
+                ts(ok, ap(ok, i0, i1), D, ap(lim), AL.is_le, None, None, [Dp, lim], YW, boost=20)
+                oky = mk(ok["b"], ok["lo"] + i0, YW)
+                oky["wr"] = ok["wr"][-1:]
+                Cp = ps(2 + y)
+                mms(Cp, [oky, Tri], [(ap(Cp, 0, YW), ap(Tri), ap(oky), True, True, YW)], boost=20)
+                tt(FI, ap(FI, i0, i1), ap(Cp, 0, YW), ap(oky), AL.is_lt, [Cp, oky], YW, boost=20)
+                FIy = mk(FI["b"], FI["lo"] + i0, YW)
+                FIy["wr"] = FI["wr"][-1:]
+                tt(Q, ap(Q, i0, i1), ap(FIy), ap(NBh, i0, i1), AL.mult, [FIy, NBh], YW, 2)
+                tt(Q, ap(Q, L + i0, L + i1), ap(Wp, i0, i1), ap(FIy), AL.mult, [FIy, Wp], YW)
+            cp = ps(1)
+            mms(cp, [FI, Zk], [(ap(cp, 0, C), Z(Zk, r), ap(FI, r, L, 16), r == 0, r == 15, C) for r in range(16)])
+            x1, x2, nf = tile("i32", C), tile("i32", C), tile("f32", C)
+            tt(x1, ap(x1), ap(cp, 0, C), ap(pw1, 0, C), AL.add, [cp, pw1], C)
+            ts(x2, ap(x2), ap(x1), 15, AL.bitwise_and, None, None, [x1], C)
+            ts(nf, ap(nf), ap(cp, 0, C), 16.0, AL.is_lt, None, None, [cp], C)
+            Qp = ps(7)
+            mms(Qp, [Q, Zh], [(ap(Qp, 0, 2 * C), Z(Zh, r), ap(Q, r, 2 * L, 16), r == 0, r == 15, 2 * C) for r in range(16)])
+            if not last:
+                Uh, ho, hp = tile("f32", C), tile("f32", 2 * C), tile("f32", 2 * C)
+                tcopy(ho, ap(ho, 0, C), ap(x2), [x2], C)
+                tt(Uh, ap(Uh), ap(nf), hUa, AL.mult, [nf, hU], C)
+                tt(ho, ap(ho, C, 2 * C), ap(Qp, 0, C), ap(Uh), AL.add, [Qp, Uh], C)
+                send(ho, ap(ho), [(hp, ap(hp), 1)])
+            Ue, Re, Ll = tile("f32", C), tile("f32", C), tile("u16", C)
+            tt(Ue, ap(Ue), ap(nf), ap(I2), AL.mult, [nf, I2], C)
+            tt(Re, ap(Re), ap(Qp, C, 2 * C), ap(Ue), AL.add, [Qp, Ue], C)
+            iL = ts(Ll, ap(Ll), ap(Re), 1536.0, AL.add, None, None, [Re], C)
+            an, a2 = tile("bf", L), tile("bf", L)
+            act(an, ap(an), ap(XB).indirect(ap(Ll)), AF.Copy, [X, ext, Ll], dur=gc_(L))
+            send(an, ap(an), [(a2, ap(a2), 1 if not last else -2)])
+            cn = ps(4)
+            mms(cn, [ok, Blk], [(ap(cn, 0, L), ap(Blk), ap(ok), True, True, L)])
+            fl, acc, P4 = tile("bf", L), tile("f32", 1), tile("hf", L)
+            act(fl, ap(fl), ap(cn, 0, L), AF.Relu, [cn], L, scale=-1.0, bias=1.0, acc=acc)
+            soft(tt(P4, ap(P4), ap(fl), ap(nM), AL.mult, [fl, nM], L, 2), iL)
+            if not last:
+                vn, vi, fi = tile("hf", L), tile("hf", L), tile("bf", L)
+                tt(vn, ap(vn), ap(P4), ap(Q, L, 2 * L), AL.add, [P4, Q], L, 2)
+                send(fl, ap(fl), [(fi, ap(fi), 2 - t)])
+                send(vn, ap(vn), [(vi, ap(vi), 2 - t)])
+                vs.append([(vi, 0)])
+                fs.append(fi)
+            else:
+                vs.append([(P4, 0), (Q, L)])
+                fs.append(fl)
+            pf, pl = tile("f32", C), tile("u16", C)
+            tt(pf, ap(pf), ap(x2), ap(xi), AL.add, [x2, xi], C)
+            tcopy(pl, ap(pl), ap(pf), [pf], C)
+
+            def put(pl=pl, an=an):
+                return [g.vector.tensor_copy(ap(X).indirect(ap(pl)), ap(an))]
+            task("V", gc_(L, "scatter"), [pl, an], [X], put)
+            if not (gen == GENS - 1 and last):
+                Ap = ps(5)
+                mms(Ap, [acc, RS], [(ap(Ap, 0, 1), ap(RS), ap(acc), True, True, 1)], 4)
+                A1, A2, lim = tile("i32", 1), tile("i32", 1), tile("f32", 1)
+                soft(tcopy(A1, ap(A1), ap(Ap, 0, 1), [Ap], 1), iL)
+                ts(A2, ap(A2), ap(A1), 63, AL.bitwise_and, None, None, [A1], 1)
+                ts(lim, ap(lim), ap(A2), ap(thf), AL.add, None, None, [A2, thf], 1)
+            a = a2
+        Ep = ps(5)
+        mms(Ep, fs + [Idb], [(ap(Ep, 0, L), ap(Idb), ap(fs[t]), t == 0, t == ST - 1, L) for t in range(ST)])
+        oh, cum = tile("bf", L), tile("bf", L)
+        ts(oh, ap(oh), ap(Ep, 0, L), ap(scol), AL.is_equal, None, None, [Ep, scol], L)
+
+        def scan(oh=oh, cum=cum):
+            return [g.vector.tensor_tensor_scan(ap(cum), ap(ones), ap(oh), 0.0, AL.mult, AL.add)]
+        task("V", vc(L, 0.5), [oh, ones], [cum], scan)
+        bp = ps(1)
+        mms(bp, [cum, Tri], [(ap(bp, 0, 1), ap(Tri), ap(cum, L - 1, L), True, True, 1)])
+        q1, q2, bs = tile("bf", L), tile("bf", L), tile("f32", 1)
+        act(bs, ap(bs), ap(bp, 0, 1), AF.Copy, [bp], 1)
+        tt(q1, ap(q1), ap(oh), ap(cum), AL.mult, [oh, cum], L, 2)
+        ts(q2, ap(q2), ap(oh), ap(bs), AL.mult, None, None, [oh, bs], L, 0.5)
+        op_ = ps(7)
+        mms(op_, [q1, q2, Zb], [(ap(op_, 0, 12), Z(Zb, r), ap(q, r, L, 16), r == 0 and q is q1, r == 15 and q is q2, 12) for q in (q1, q2) for r in range(16)])
+        po = tile("u16", 12)
+        ts(po, ap(po), ap(op_, 0, 12), -1.0, AL.add, None, None, [op_], 12)
+        dp, lst = ps(6), [(ap(Idh), ap(mother))]
+        for t in range(ST):
+            lst += [(ap(Lt[t]), ap(v, o, o + L)) for v, o in vs[t]]
+        lst = [(ap(dp, 0, L), l, r, j == 0, j == len(lst) - 1, L) for j, (l, r) in enumerate(lst)]
+        mms(dp, [mother, Idh] + Lt + [v for w in vs for v, _ in w], lst)
+        dau, srt = tile("f32", L), tile("f32", L)
+        act(dau, ap(dau), ap(dp, 0, L), AF.Copy, [dp], L)
+
+        def scat(srt=srt, po=po, dau=dau):
+            return [g.vector.tensor_copy(ap(srt).indirect(ap(po)), ap(dau))]
+        y1, y2, y3, y4 = tile("f32", 12), tile("f32", 12), tile("f32", 12), tile("f32", 12)
+        ts(y1, ap(y1), ap(op_, 0, 12), 145.0, AL.is_ge, None, None, [op_], 12)
+        tt(y2, ap(y2), ap(i144), ap(op_, 0, 12), AL.subtract, [i144, op_], 12)
+        tt(y3, ap(y3), ap(y1), ap(y2), AL.mult, [y1, y2], 12)
+        tt(y4, ap(y4), ap(y3), ap(i48), AL.add, [y3, i48], 12)
+        Lm, Ln, prev = tile("f32", 12), tile("u16", 12), tile("f32", 48)
+        send(y4, ap(y4), [(Lm, ap(Lm), -2)])
+        task("V", gc_(L, "scatter"), [po, dau], [srt], scat)
+        best = mk(srt["b"], srt["lo"], 48)
+        best["wr"] = srt["wr"]
+        send(best, ap(best), [(own, ap(own, 0, 48), -2), (prev, ap(prev), -1)])
+        tcopy(Ln, ap(Ln), ap(Lm), [Lm], 12)
+        own2 = mk(own["b"], own["lo"], own["n"])
+        own2["wr"] = list(own["wr"])
+        tcopy(own2, ap(own, 1, 48, 2), ap(prev, 1, 48, 2), [own, prev], 24)
+        new = tile("f32", 48 + L)
+        tcopy(new, ap(new, 48, 48 + L), ap(own).indirect(ap(Ln)), [own2, Ln], dur=gc_(L))
+        if gen < GENS - 1:
+            tcopy(G, ap(G, 0, GW, 8), ap(new, 48, 48 + L), [new], L)
+        own = new
+    yo, ao, so = tile("f32", L), tile("f32", L), tile("f32", L)
+    act(yo, ap(yo), ap(own, 48, 48 + L), AF.Copy, [own], L, bias=1536.0)
+    store(T.yg[:], ap(yo), [yo])
+    act(ao, ap(ao), ap(a), AF.Copy, [a], L)
+    store(T.ya[:], ap(ao), [ao])
+    sp = ps(0)
+    mms(sp, [X, Idb], [(ap(sp, 0, L), ap(Idb), ap(X, s, XW, 16), s == 0, s == 15, L) for s in range(16)])
+    act(so, ap(so), ap(sp, 0, L), AF.Copy, [sp], L)
+    store(T.ys[:], ap(so), [so])
+    emit(g, T, tasks)
+
+
+def tid(d):
+    return d[0] if isinstance(d, tuple) else d
+
+
+def order(tasks):
+    n = len(tasks)
+    succ, left = [[] for _ in range(n)], [0] * n
+    for i, t in enumerate(tasks):
+        for d, lag in t["deps"].items():
+            succ[tid(d)].append((i, lag))
+        left[i] = len(t["deps"])
+    prio, seen = [0.0] * n, set()
+
+    def visit(i):
+        stack = [i]
+        while stack:
+            j = stack[-1]
+            if j in seen:
+                stack.pop()
+                continue
+            more = [k for k, _ in succ[j] if k not in seen]
+            if more:
+                stack += more
+                continue
+            prio[j] = tasks[j]["dur"] + max([prio[k] + COST["sem"] + lag for k, lag in succ[j]], default=0.0)
+            seen.add(j)
+            stack.pop()
+    for i in range(n):
+        visit(i)
+    free, fin, out = {}, [0.0] * n, []
+    avail = {i: 0.0 for i in range(n) if not left[i]}
+    while avail:
+        st, _, i = min((max(r, free.get(tasks[i]["q"], 0.0)), -prio[i] - tasks[i]["boost"], i) for i, r in avail.items())
+        del avail[i]
+        fin[i] = free[tasks[i]["q"]] = st + tasks[i]["dur"]
+        out.append(i)
+        for j, _ in succ[i]:
+            left[j] -= 1
+            if not left[j]:
+                avail[j] = max(fin[tid(d)] + lag + COST["sem"] for d, lag in tasks[j]["deps"].items())
+    return out
+
+
+def emit(g, T, tasks):
+    eng = {"V": g.vector, "S": g.scalar, "P": g.tensor, "G": g, "Y": g.sync}
+    sem_of = {"V": "sV", "S": "sS", "P": "sP", "G": "sG"}
+    count = {s: 0 for s in sem_of.values()}
+    known, done = {q: {} for q in eng}, {}
+    sent, ends = 0, []
+    for i in order(tasks):
+        t = tasks[i]
+        q = t["q"]
+        k, need = known[q], {}
+        for d in t["deps"]:
+            if d in t["soft"]:
+                continue
+            s, v, kn = done[d]
+            if k.get(s, 0) < v and need.get(s, (0, None))[0] < v:
+                need[s] = (v, kn)
+        for s in sorted(need, key=lambda s: -len(need[s][1])):
+            v, kn = need[s]
+            if k.get(s, 0) >= v or any(o != s and need[o][1].get(s, 0) >= v and k.get(o, 0) < need[o][0] for o in need):
+                continue
+            eng[q].wait_ge(T.sem[s], v)
+            for b, w in kn.items():
+                k[b] = max(k.get(b, 0), w)
+            k[s] = max(v, k.get(s, 0))
+        for s, (v, kn) in need.items():
+            if k.get(s, 0) < v:
+                eng[q].wait_ge(T.sem[s], v)
+                k[s] = v
+        ins = t["fn"]()
+        if t["kind"] == "c":
+            s = sem_of[q]
+            for m in ins:
+                m.then_inc(T.sem[s], 1)
+            count[s] += len(ins)
+            done[i] = (s, count[s], dict(k))
+        elif t["kind"] == "d":
+            s = "d%d" % t["x"]
+            ins[0].then_inc(T.sem[s], 16)
+            done[i] = (s, 16, dict(k))
+            ends.append((s, 16))
+        else:
+            got, out = t["x"]
+            sent += out
+            for m, (name, c) in enumerate(got):
+                done[(i, m)] = (name, c, {})
+                ends.append((name, c))
+    for s, v in ends + [("left", sent)] + list(count.items()):
+        if known["Y"].get(s, 0) < v:
+            g.sync.wait_ge(T.sem[s], v)

@@ -2,11 +2,12 @@ from concourse.bass import DstId, RemoteDMATransfer
 from concourse.mybir import AluOpType, ActivationFunctionType
 
 AL, AF = AluOpType, ActivationFunctionType
-NR, L, ST, GENS, KR = 8, 192, 3, 2, 48
+NR, L, ST, GENS = 8, 192, 3, 2
 GW, XW = 1536, 3072
 C = 12
 EC, CW = 4, 48
-YC, YW, KG = 2, 96, 4
+NC, W, KG = 2, 96, 4
+SM = 4
 VG = "SSSV"
 POOL = {"f32": ("float32", 11000), "bf": ("bfloat16", 28000), "hf": ("float16", 15000), "u16": ("uint16", 4600), "i32": ("int32", 3600)}
 SIZE = {"f32": 4, "bf": 2, "hf": 2, "u16": 2, "i32": 4}
@@ -128,10 +129,10 @@ def rank_program(g, core, T, topo):
         if after:
             for w, _ in after["wr"][:-1]:
                 soft(i, w)
+        return i
 
-    def load(q, out, oa, src, dur):
-        e = g.sync if q == "Y" else g.scalar
-        i = task(q, 0.1, [], [out], lambda: [e.dma_start(oa, src)], "d", ndma[0])
+    def load(out, oa, src, dur):
+        i = task("Y", 0.1, [], [out], lambda: [g.sync.dma_start(oa, src)], "d", ndma[0])
         out["wr"] = [(w, dur if w == i else lg) for w, lg in out["wr"]]
         ndma[0] += 1
 
@@ -167,16 +168,21 @@ def rank_program(g, core, T, topo):
         i = task("G", COST["issue"], [src], [], fn, "r", (got, sum(out)), boost)
         for m, (dst, da, d) in enumerate(moves):
             dst["wr"].append(((i, m), COST["hop"] + src["n"] * 512 / 60000.0))
+        return i
 
     gni, nbi, thi = tile("i32", GW), tile("i32", GW), tile("i32", 1)
     XB = tile("bf", XW + L)
     X, ext = mk(XB["b"], XB["lo"], XW, True), mk(XB["b"], XB["lo"] + XW, L, True)
     a = tile("bf", L)
-    load("Y", thi, ap(thi), T.th[:], 3.0)
-    load("Y", gni, ap(gni), T.gn[:], 5.0)
-    load("S", nbi, ap(nbi), T.nb[:], 6.5)
-    load("S", X, ap(X), T.x[:], 8.0)
-    load("Y", a, ap(a), T.a0[:], 8.0)
+    load(thi, ap(thi), T.th[:], 1.8)
+    gh = [mk(gni["b"], gni["lo"] + 768 * j, 768) for j in range(2)]
+    for j in range(2):
+        load(gh[j], ap(gh[j]), T.gn[:, 768 * j:768 * j + 768], 2.3 + 0.5 * j)
+    load(nbi, ap(nbi), T.nb[:], 3.8)
+    load(X, ap(X), T.x[:], 4.8)
+    load(a, ap(a), T.a0[:], 4.8)
+    for i in range(1, len(tasks)):
+        soft(i, i - 1)
 
     def col(ins, src, s1, op0, s2=None, op1=None, n=1, pool="f32", f=1.0):
         t = tile(pool, n)
@@ -212,6 +218,7 @@ def rank_program(g, core, T, topo):
     Zb = col([im, zc], ap(im), ap(zc), AL.is_equal, n=144, pool="bf")
     Zk = col([Zh, k16], ap(Zh), ap(k16), AL.mult, n=144, pool="hf", f=0.5)
     Idb = col([im, pcol], ap(im, 0, 128), ap(pcol), AL.is_equal, n=128, pool="bf")
+    Im = col([Idb], ap(Idb), -1.0, AL.mult, n=128, pool="bf", f=0.5)
     Blk = col([mgf, gcol], ap(mgf), ap(gcol), AL.is_equal, n=128, pool="bf")
     lt = col([im, pcol], ap(im, 0, 128), ap(pcol), AL.is_gt, n=128, pool="bf")
     Tri = tile("bf", 128)
@@ -237,8 +244,10 @@ def rank_program(g, core, T, topo):
     El0 = tile("u16", L)
     tcopy(El0, ap(El0), own_nb, [nbi], L)
     NBh0 = col([nbi], own_nb, -1536.0, AL.add, n=L)
-    G = tile("f32", GW, True)
-    ts(G, ap(G), ap(gni), -1536.0, AL.add, None, None, [gni], GW)
+    G = tile("f32", GW)
+    for j in range(2):
+        ts(G, ap(G, 768 * j, 768 * j + 768), ap(gh[j]), -1536.0, AL.add, None, None, [gh[j]], 768)
+    G["mut"] = True
     NBf = tile("f32", GW)
     for j in range(4):
         ts(NBf, ap(NBf, 384 * j, 384 * j + 384), ap(nbi, 384 * j, 384 * j + 384), -1536.0, AL.add, None, None, [nbi], 384)
@@ -251,7 +260,7 @@ def rank_program(g, core, T, topo):
     lim = thf
     for gen in range(GENS):
         mo, mother = tile("hf", L), tile("hf", L)
-        ts(mo, ap(mo), ap(own, 48, 48 + L), ap(rm3), AL.mult, None, None, [own, rm3], L, boost=-30)
+        imo = ts(mo, ap(mo), ap(own, 48, 48 + L), ap(rm3), AL.mult, None, None, [own, rm3], L, boost=-30)
         send(mo, ap(mo), [(mother, ap(mother), 2)], boost=-30)
         hp = None
         vs, fs = [], []
@@ -275,7 +284,11 @@ def rank_program(g, core, T, topo):
                 act(NBh, ap(NBh), ap(NBf).indirect(ap(hl)), AF.Copy, [NBf, hl], dur=gc_(L), boost=50)
                 ts(El, ap(El), ap(NBh), 1536.0, AL.add, None, None, [NBh], L, boost=50)
                 mask = ring("bf", 16 * L, "mask")
-                for k in range(16):
+                for k in range(16 - SM, 16):
+                    ab = ring("bf", L, ("ab", k))
+                    act(ab, ap(ab), ap(prb), AF.Abs, [prb, ck], L, scale=-1.0, bias=ap(ck, k, k + 1))
+                    act(mask, ap(mask, k, 16 * L, 16), ap(ab), AF.Relu, [ab], L, scale=-1.0, bias=1.0)
+                for k in range(16 - SM):
                     ts(mask, ap(mask, k, 16 * L, 16), ap(prb), ap(ck, k, k + 1), AL.is_equal, None, None, [prb, ck], L, 0.5)
                 inM = tt(nM, ap(nM), ap(G).indirect(ap(hl)), ap(mask, 0, 16 * L, 16), AL.mult, [G, hl, mask], dur=gc_(L))
                 hU, hUa, pw1 = hp, ap(hp, C, 2 * C), tile("f32", C)
@@ -283,13 +296,13 @@ def rank_program(g, core, T, topo):
             V, Vj, iG, iW = ring("bf", 16 * L, "V"), [], [], []
             Wp = ps(0)
             for j in range(EC):
-                Gg = ring("hf", 16 * CW, ("Gg", j))
-                m0 = 0 if t == 0 else 16 * CW * j
-                iG.append(tt(Gg, ap(Gg), ap(G).indirect(ap(El, j * CW, j * CW + CW)), ap(mask, m0, m0 + 16 * CW), AL.mult, [G, El, mask], dur=gc_(16 * CW)))
-                mms(Wp, [Gg, Zh], [(ap(Wp, j * CW, j * CW + CW), Z(Zh, k), ap(Gg, k, 16 * CW, 16), k == 0, k == 15, CW) for k in range(16)])
+                Gg, c0, c1 = ring("hf", 16 * CW, ("Gg", j)), j * CW, j * CW + CW
+                m0 = 0 if t == 0 else 16 * c0
+                iG.append(tt(Gg, ap(Gg), ap(G).indirect(ap(El, c0, c1)), ap(mask, m0, m0 + 16 * CW), AL.mult, [G, El, mask], dur=gc_(16 * CW)))
+                iWm = mms(Wp, [Gg, Zh], [(ap(Wp, c0, c1), Z(Zh, k), ap(Gg, k, 16 * CW, 16), k == 0, k == 15, CW) for k in range(16)])
                 Wl = tile("u16", CW)
-                iW.append(ts(Wl, ap(Wl), ap(Wp, j * CW, j * CW + CW), 1536.0, AL.add, None, None, [Wp], CW, boost=50))
-                Vv = mk(V["b"], V["lo"] + 16 * CW * j, 16 * CW, False, V["pre"])
+                iW.append(ts(Wl, ap(Wl), ap(Wp, c0, c1), 1536.0, AL.add, None, None, [Wp], CW, boost=50))
+                Vv = mk(V["b"], V["lo"] + 16 * c0, 16 * CW, False, V["pre"])
                 if VG[j] == "V":
                     tcopy(Vv, ap(Vv), ap(X).indirect(ap(Wl)), [X, Wl], dur=gc_(16 * CW))
                 else:
@@ -297,51 +310,58 @@ def rank_program(g, core, T, topo):
                 V["wr"] += Vv["wr"]
                 Vj.append(Vv)
                 if j == 0:
-                    npz = ps(1)
+                    npz, dq = ps(1), ps(7)
                     mms(npz, [nM, Zh], [(ap(npz, 0, C), Z(Zh, r), ap(nM, r, L, 16), r == 0, r == 15, C) for r in range(16)])
                     nl, df = tile("u16", C), tile("bf", L)
                     inl = ts(nl, ap(nl), ap(npz, 0, C), 1536.0, AL.add, None, None, [npz], C, boost=50)
-                    idf = tt(df, ap(df), ap(X).indirect(ap(nl)), ap(a), AL.subtract, [X, nl, a], dur=gc_(L), boost=50)
-                    act(ext, ap(ext), ap(df), AF.Abs, [df], L, boost=50)
-            seq = [iG[0], inM, iW[0], iG[1], inl, iW[1], iG[2], idf, iW[2], iG[3], iW[3]]
+                    act(df, ap(df), ap(X).indirect(ap(nl)), AF.Copy, [X, nl], dur=gc_(L), boost=50)
+                    mms(dq, [df, a, Idb, Im], [(ap(dq, 0, L), ap(Idb), ap(df), True, False, L), (ap(dq, 0, L), ap(Im), ap(a), False, True, L)], boost=50)
+                    act(ext, ap(ext), ap(dq, 0, L), AF.Abs, [dq], L, boost=50)
+            seq = [iG[0], inM, iW[0], iG[1], inl, iW[1], iG[2], iW[2], iG[3], iW[3]]
+            if t == 0:
+                soft(imo, iG[0])
             for u, v in zip(seq, seq[1:]):
                 soft(v, u)
             FI, Q, ok = tile("hf", L), tile("hf", 2 * L), tile("bf", L)
-            for y in range(YC):
-                i0, i1 = y * YW, y * YW + YW
-                vin = [Vj[j] for j in range(EC) if i0 <= j * CW < i1]
+            for y in range(NC):
+                i0, i1 = y * W, y * W + W
                 Dp = ps(2 + y)
-                D = ap(Dp, 0, YW)
+                D = ap(Dp, 0, W)
                 Te = ap(ext, i0, i1)
+                vin = [Vj[j] for j in range(EC) if i0 <= j * CW < i1]
                 for q in range(16 // KG):
                     Y, lst, dl = ps(4 + (y * 4 + q) % 3), [], []
-                    ya = ring("bf", KG * YW, ("ya", y, q))
+                    ya = ring("bf", KG * W, ("ya", y, q))
                     for kk in range(KG):
                         k = q * KG + kk
-                        o, v = ap(Y, kk * YW, kk * YW + YW), ap(V, 16 * i0 + k, 16 * i1, 16)
-                        lst += [(o, ap(Idb), v, True, False, YW), (o, ap(Idb), Te, False, True, YW)]
-                        dl.append((D, Z(Zb, k), ap(ya, kk * YW, kk * YW + YW), k == 0, k == 15, YW))
+                        o, v = ap(Y, kk * W, kk * W + W), ap(V, 16 * i0 + k, 16 * i1, 16)
+                        lst += [(o, ap(Idb), v, True, False, W), (o, ap(Idb), Te, False, True, W)]
+                        dl.append((D, Z(Zb, k), ap(ya, kk * W, kk * W + W), k == 0, k == 15, W))
                     mms(Y, vin + [Idb, ext], lst)
-                    act(ya, ap(ya), ap(Y, 0, KG * YW), AF.Abs, [Y], KG * YW, bias=-255.0)
-                    mms(Dp, [ya, Zb], dl, after=Dp, boost=20)
-                ts(ok, ap(ok, i0, i1), D, ap(lim), AL.is_le, None, None, [Dp, lim], YW, boost=20)
-                oky = mk(ok["b"], ok["lo"] + i0, YW)
+                    act(ya, ap(ya), ap(Y, 0, KG * W), AF.Abs, [Y], KG * W, bias=-255.0)
+                    soft(mms(Dp, [ya, Zb], dl, after=Dp, boost=20), iWm)
+                ts(ok, ap(ok, i0, i1), D, ap(lim), AL.is_le, None, None, [Dp, lim], W, boost=20)
+                oky = mk(ok["b"], ok["lo"] + i0, W)
                 oky["wr"] = ok["wr"][-1:]
                 Cp = ps(2 + y)
-                mms(Cp, [oky, Tri], [(ap(Cp, 0, YW), ap(Tri), ap(oky), True, True, YW)], boost=20)
-                tt(FI, ap(FI, i0, i1), ap(Cp, 0, YW), ap(oky), AL.is_lt, [Cp, oky], YW, boost=20)
-                FIy = mk(FI["b"], FI["lo"] + i0, YW)
+                mms(Cp, [oky, Tri], [(ap(Cp, 0, W), ap(Tri), ap(oky), True, True, W)], boost=20)
+                tt(FI, ap(FI, i0, i1), ap(Cp, 0, W), ap(oky), AL.is_lt, [Cp, oky], W, boost=20)
+                FIy = mk(FI["b"], FI["lo"] + i0, W)
                 FIy["wr"] = FI["wr"][-1:]
-                tt(Q, ap(Q, i0, i1), ap(FIy), ap(NBh, i0, i1), AL.mult, [FIy, NBh], YW, 2)
-                tt(Q, ap(Q, L + i0, L + i1), ap(Wp, i0, i1), ap(FIy), AL.mult, [FIy, Wp], YW)
+                tt(Q, ap(Q, i0, i1), ap(FIy), ap(NBh, i0, i1), AL.mult, [FIy, NBh], W, 2)
+                tt(Q, ap(Q, L + i0, L + i1), ap(Wp, i0, i1), ap(FIy), AL.mult, [FIy, Wp], W)
             cp = ps(1)
             mms(cp, [FI, Zk], [(ap(cp, 0, C), Z(Zk, r), ap(FI, r, L, 16), r == 0, r == 15, C) for r in range(16)])
             x1, x2, nf = tile("i32", C), tile("i32", C), tile("f32", C)
-            tt(x1, ap(x1), ap(cp, 0, C), ap(pw1, 0, C), AL.add, [cp, pw1], C)
+            icode = tt(x1, ap(x1), ap(cp, 0, C), ap(pw1, 0, C), AL.add, [cp, pw1], C)
             ts(x2, ap(x2), ap(x1), 15, AL.bitwise_and, None, None, [x1], C)
-            ts(nf, ap(nf), ap(cp, 0, C), 16.0, AL.is_lt, None, None, [cp], C)
-            Qp = ps(7)
-            mms(Qp, [Q, Zh], [(ap(Qp, 0, 2 * C), Z(Zh, r), ap(Q, r, 2 * L, 16), r == 0, r == 15, 2 * C) for r in range(16)])
+            soft(ts(nf, ap(nf), ap(cp, 0, C), 16.0, AL.is_lt, None, None, [cp], C), icode)
+            Qp, Qe = ps(7), ps(3)
+            for Qx, o in ((Qp, 0), (Qe, L)):
+                if Qx is Qe or not last:
+                    Qs = mk(Q["b"], Q["lo"] + o, L)
+                    Qs["wr"] = Q["wr"][o // L::2]
+                    mms(Qx, [Qs, Zh], [(ap(Qx, 0, C), Z(Zh, r), ap(Qs, r, L, 16), r == 0, r == 15, C) for r in range(16)])
             if not last:
                 Uh, ho, hp = tile("f32", C), tile("f32", 2 * C), tile("f32", 2 * C)
                 tcopy(ho, ap(ho, 0, C), ap(x2), [x2], C)
@@ -350,20 +370,21 @@ def rank_program(g, core, T, topo):
                 send(ho, ap(ho), [(hp, ap(hp), 1)])
             Ue, Re, Ll = tile("f32", C), tile("f32", C), tile("u16", C)
             tt(Ue, ap(Ue), ap(nf), ap(I2), AL.mult, [nf, I2], C)
-            tt(Re, ap(Re), ap(Qp, C, 2 * C), ap(Ue), AL.add, [Qp, Ue], C)
+            tt(Re, ap(Re), ap(Qe, 0, C), ap(Ue), AL.add, [Qe, Ue], C)
             iL = ts(Ll, ap(Ll), ap(Re), 1536.0, AL.add, None, None, [Re], C)
             an, a2 = tile("bf", L), tile("bf", L)
             act(an, ap(an), ap(XB).indirect(ap(Ll)), AF.Copy, [X, ext, Ll], dur=gc_(L))
-            send(an, ap(an), [(a2, ap(a2), 1 if not last else -2)])
+            ian = send(an, ap(an), [(a2, ap(a2), 1 if not last else -2)])
             cn = ps(4)
-            mms(cn, [ok, Blk], [(ap(cn, 0, L), ap(Blk), ap(ok), True, True, L)])
+            mms(cn, [ok, Blk], [(ap(cn, 0, L), ap(Blk), ap(ok), True, True, L)], boost=40 if last else 0)
             fl, acc, P4 = tile("bf", L), tile("f32", 1), tile("hf", L)
             act(fl, ap(fl), ap(cn, 0, L), AF.Relu, [cn], L, scale=-1.0, bias=1.0, acc=acc)
-            soft(tt(P4, ap(P4), ap(fl), ap(nM), AL.mult, [fl, nM], L, 2), iL)
+            iP4 = tt(P4, ap(P4), ap(fl), ap(nM), AL.mult, [fl, nM], L, 2)
             if not last:
+                soft(iP4, iL)
                 vn, vi, fi = tile("hf", L), tile("hf", L), tile("bf", L)
                 tt(vn, ap(vn), ap(P4), ap(Q, L, 2 * L), AL.add, [P4, Q], L, 2)
-                send(fl, ap(fl), [(fi, ap(fi), 2 - t)])
+                soft(send(fl, ap(fl), [(fi, ap(fi), 2 - t)]), ian)
                 send(vn, ap(vn), [(vi, ap(vi), 2 - t)])
                 vs.append([(vi, 0)])
                 fs.append(fi)
@@ -376,9 +397,9 @@ def rank_program(g, core, T, topo):
 
             def put(pl=pl, an=an):
                 return [g.vector.tensor_copy(ap(X).indirect(ap(pl)), ap(an))]
-            task("V", gc_(L, "scatter"), [pl, an], [X], put)
+            iput = task("V", gc_(L, "scatter"), [pl, an], [X], put)
             if not (gen == GENS - 1 and last):
-                Ap = ps(5)
+                Ap = ps(0)
                 mms(Ap, [acc, RS], [(ap(Ap, 0, 1), ap(RS), ap(acc), True, True, 1)], 4)
                 A1, A2, lim = tile("i32", 1), tile("i32", 1), tile("f32", 1)
                 soft(tcopy(A1, ap(A1), ap(Ap, 0, 1), [Ap], 1), iL)
@@ -386,21 +407,23 @@ def rank_program(g, core, T, topo):
                 ts(lim, ap(lim), ap(A2), ap(thf), AL.add, None, None, [A2, thf], 1)
             a = a2
         Ep = ps(5)
-        mms(Ep, fs + [Idb], [(ap(Ep, 0, L), ap(Idb), ap(fs[t]), t == 0, t == ST - 1, L) for t in range(ST)])
+        mms(Ep, fs + [Idb], [(ap(Ep, 0, L), ap(Idb), ap(fs[t]), t == 0, t == ST - 1, L) for t in range(ST)], boost=40)
         oh, cum = tile("bf", L), tile("bf", L)
-        ts(oh, ap(oh), ap(Ep, 0, L), ap(scol), AL.is_equal, None, None, [Ep, scol], L)
+        ts(oh, ap(oh), ap(Ep, 0, L), ap(scol), AL.is_equal, None, None, [Ep, scol], L, boost=40)
 
         def scan(oh=oh, cum=cum):
             return [g.vector.tensor_tensor_scan(ap(cum), ap(ones), ap(oh), 0.0, AL.mult, AL.add)]
-        task("V", vc(L, 0.5), [oh, ones], [cum], scan)
-        bp = ps(1)
-        mms(bp, [cum, Tri], [(ap(bp, 0, 1), ap(Tri), ap(cum, L - 1, L), True, True, 1)])
-        q1, q2, bs = tile("bf", L), tile("bf", L), tile("f32", 1)
-        act(bs, ap(bs), ap(bp, 0, 1), AF.Copy, [bp], 1)
-        tt(q1, ap(q1), ap(oh), ap(cum), AL.mult, [oh, cum], L, 2)
-        ts(q2, ap(q2), ap(oh), ap(bs), AL.mult, None, None, [oh, bs], L, 0.5)
+        task("V", vc(L, 0.5), [oh, ones], [cum], scan, boost=40)
+        bp = ps(5)
+        mms(bp, [cum, Tri], [(ap(bp, 0, 1), ap(Tri), ap(cum, L - 1, L), True, True, 1)], boost=40)
+        q1, q2 = tile("bf", L), tile("bf", L)
+        tt(q1, ap(q1), ap(oh), ap(cum), AL.mult, [oh, cum], L, 2, boost=40)
+        iq2 = ts(q2, ap(q2), ap(oh), ap(bp, 0, 1), AL.mult, None, None, [oh, bp], L, 0.5, boost=40)
+        soft(iP4, iq2)
+        soft(icode, iP4)
         op_ = ps(7)
-        mms(op_, [q1, q2, Zb], [(ap(op_, 0, 12), Z(Zb, r), ap(q, r, L, 16), r == 0 and q is q1, r == 15 and q is q2, 12) for q in (q1, q2) for r in range(16)])
+        for q in (q1, q2):
+            mms(op_, [q, Zb], [(ap(op_, 0, 12), Z(Zb, r), ap(q, r, L, 16), r == 0 and q is q1, r == 15 and q is q2, 12) for r in range(16)], boost=40, after=op_)
         po = tile("u16", 12)
         ts(po, ap(po), ap(op_, 0, 12), -1.0, AL.add, None, None, [op_], 12)
         dp, lst = ps(6), [(ap(Idh), ap(mother))]
@@ -417,13 +440,15 @@ def rank_program(g, core, T, topo):
         ts(y1, ap(y1), ap(op_, 0, 12), 145.0, AL.is_ge, None, None, [op_], 12)
         tt(y2, ap(y2), ap(i144), ap(op_, 0, 12), AL.subtract, [i144, op_], 12)
         tt(y3, ap(y3), ap(y1), ap(y2), AL.mult, [y1, y2], 12)
-        tt(y4, ap(y4), ap(y3), ap(i48), AL.add, [y3, i48], 12)
+        iy4 = tt(y4, ap(y4), ap(y3), ap(i48), AL.add, [y3, i48], 12)
         Lm, Ln, prev = tile("f32", 12), tile("u16", 12), tile("f32", 48)
         send(y4, ap(y4), [(Lm, ap(Lm), -2)])
-        task("V", gc_(L, "scatter"), [po, dau], [srt], scat)
+        isc = task("V", gc_(L, "scatter"), [po, dau], [srt], scat)
+        soft(isc, iy4)
+        soft(iput, isc)
         best = mk(srt["b"], srt["lo"], 48)
         best["wr"] = srt["wr"]
-        send(best, ap(best), [(own, ap(own, 0, 48), -2), (prev, ap(prev), -1)])
+        soft(ian, send(best, ap(best), [(own, ap(own, 0, 48), -2), (prev, ap(prev), -1)]))
         tcopy(Ln, ap(Ln), ap(Lm), [Lm], 12)
         own2 = mk(own["b"], own["lo"], own["n"])
         own2["wr"] = list(own["wr"])
@@ -456,24 +481,16 @@ def order(tasks):
         for d, lag in t["deps"].items():
             succ[tid(d)].append((i, lag))
         left[i] = len(t["deps"])
-    prio, seen = [0.0] * n, set()
-
-    def visit(i):
-        stack = [i]
-        while stack:
-            j = stack[-1]
-            if j in seen:
-                stack.pop()
-                continue
-            more = [k for k, _ in succ[j] if k not in seen]
-            if more:
-                stack += more
-                continue
-            prio[j] = tasks[j]["dur"] + max([prio[k] + COST["sem"] + lag for k, lag in succ[j]], default=0.0)
-            seen.add(j)
-            stack.pop()
-    for i in range(n):
-        visit(i)
+    need, topo_order = list(left), [i for i in range(n) if not left[i]]
+    for i in topo_order:
+        for j, _ in succ[i]:
+            need[j] -= 1
+            if not need[j]:
+                topo_order.append(j)
+    assert len(topo_order) == n
+    prio = [0.0] * n
+    for i in reversed(topo_order):
+        prio[i] = tasks[i]["dur"] + max([prio[j] + COST["sem"] + lag for j, lag in succ[i]], default=0.0)
     free, fin, out = {}, [0.0] * n, []
     avail = {i: 0.0 for i in range(n) if not left[i]}
     while avail:

from concourse.bass import DstId, RemoteDMATransfer
from concourse.mybir import AluOpType, ActivationFunctionType

AL, AF = AluOpType, ActivationFunctionType
NR, L, ST, GENS = 8, 192, 3, 2
GW, XW = 1536, 3072
C = 12
EC, CW = 4, 48
NC, W, KG = 2, 96, 4
SM = 4
VG = "SSSV"
POOL = {"f32": ("float32", 11000), "bf": ("bfloat16", 28000), "hf": ("float16", 15000), "u16": ("uint16", 4600), "i32": ("int32", 3600)}
SIZE = {"f32": 4, "bf": 2, "hf": 2, "u16": 2, "i32": 4}
SCRATCH = {"p_" + k: ("sbuf", [128, v[1]], v[0]) for k, v in POOL.items()}
SCRATCH.update({"bank%d" % b: ("psum", [128, 512], "float32") for b in range(8)})
SEMAPHORES = ["sV", "sS", "sP", "sG", "left"] + ["d%d" % i for i in range(10)] + ["r%d" % i for i in range(40)]
CY = 0.00083
COST = {"f": 1.25, "gather": 1.56, "scatter": 3.5, "issue": 0.9, "hop": 2.2, "sem": 0.06, "pe": 0.00042}


def rank_program(g, core, T, topo):
    rank = T.rank_of(core)
    if rank is None:
        return
    tasks, used, rings = [], {k: 0 for k in POOL}, {}
    bank_use = [dict() for _ in range(8)]
    ndma, nrem = [0], [0]

    def mk(b, lo, n, mut=False, pre=()):
        return {"b": b, "lo": lo, "n": n, "wr": [], "rd": [], "mut": mut, "pre": pre}

    def tile(pool, n, mut=False):
        lo, al = used[pool], 32 // SIZE[pool]
        used[pool] = (lo + n + al - 1) // al * al
        assert used[pool] <= POOL[pool][1]
        return mk("p_" + pool, lo, n, mut)

    def ring(pool, n, key):
        if key not in rings:
            rings[key] = tile(pool, n)
        else:
            o = rings[key]
            rings[key] = mk(o["b"], o["lo"], n, False, [i for i, _ in o["wr"]] + o["rd"])
        return rings[key]

    def ps(bank):
        t = mk("bank%d" % bank, 0, 512)
        t["bank"] = bank
        return t

    def ap(t, a=0, b=None, st=1):
        b = t["n"] if b is None else b
        buf = T[t["b"]]
        return buf[:, t["lo"] + a:t["lo"] + b] if st == 1 else buf[:, t["lo"] + a:t["lo"] + b:st]

    def task(q, dur, ins, outs, fn, kind="c", extra=None, boost=0.0):
        i, deps = len(tasks), {}
        for t in ins:
            for w, lag in t["wr"]:
                deps[w] = max(deps.get(w, 0), lag)
        for t in outs:
            for w in t["pre"]:
                deps.setdefault(w, 0)
            if t["mut"]:
                for w, lag in t["wr"]:
                    deps[w] = max(deps.get(w, 0), lag)
                for r in t["rd"]:
                    deps.setdefault(r, 0)
        for t in list(ins) + list(outs):
            if "bank" in t:
                bu = bank_use[t["bank"]]
                for q2 in list(bu):
                    if q2 != q:
                        for j in bu[q2]:
                            deps.setdefault(j, 0)
                        bu[q2] = []
                if i not in bu.setdefault(q, []):
                    bu[q].append(i)
        deps.pop(i, None)
        tasks.append({"q": q, "dur": dur, "deps": deps, "fn": fn, "kind": kind, "x": extra, "soft": set(), "boost": boost})
        for t in outs:
            if t["mut"]:
                t["wr"], t["rd"] = [], []
            t["wr"].append((i, 0))
        for t in ins:
            t["rd"].append(i)
        return i

    def soft(i, j):
        if j not in tasks[i]["deps"]:
            tasks[i]["deps"][j] = 0
            tasks[i]["soft"].add(j)

    def vc(n, f=1.0):
        return (0.05 + max(64, n * f) * CY) * COST["f"]

    def gc_(n, k="gather"):
        return (0.06 + n * COST[k] * CY) * COST["f"]

    def ts(out, oa, in0, s1, op0, s2, op1, ins, n, f=1.0, boost=0.0):
        def fn():
            if op1 is None:
                return [g.vector.tensor_scalar(oa, in0, s1, None, op0)]
            return [g.vector.tensor_scalar(oa, in0, s1, s2, op0, op1)]
        return task("V", vc(n, f), ins, [out], fn, boost=boost)

    def tt(out, oa, in0, in1, op, ins, n=0, f=1.0, dur=None, boost=0.0):
        return task("V", vc(n, f) if dur is None else dur, ins, [out], lambda: [g.vector.tensor_tensor(oa, in0, in1, op)], boost=boost)

    def tcopy(out, oa, in0, ins, n=0, f=1.0, dur=None):
        return task("V", vc(n, f) if dur is None else dur, ins, [out], lambda: [g.vector.tensor_copy(oa, in0)])

    def act(out, oa, in0, func, ins, n=0, dur=None, bias=0.0, scale=1.0, acc=None, boost=0.0):
        return task("S", vc(n) if dur is None else dur, ins, [out] + ([acc] if acc else []),
                    lambda: [g.scalar.activation(oa, in0, func, bias=bias, scale=scale, accum_out=ap(acc) if acc else None)], boost=boost)

    def iota(out, pat, base, cm, flag=True):
        task("G", 0.13 + 2 * out["n"] * CY, [], [out], lambda: [g.iota(ap(out), pat, base, cm, allow_small_or_imprecise_dtypes=flag)])

    def mms(out, ins, lst, f32=1, boost=0.0, after=None):
        def fn():
            r = []
            for o, l, x, a, b, n in lst:
                m = g.tensor.matmul(o, l, x, a, b)
                if b:
                    r.append(m)
            return r or [m]
        i = task("P", (0.03 + sum(max(64, m[5]) for m in lst) * COST["pe"] * f32) * COST["f"], ins, [out], fn, boost=boost)
        if after:
            for w, _ in after["wr"][:-1]:
                soft(i, w)
        return i

    def load(out, oa, src, dur):
        i = task("Y", 0.1, [], [out], lambda: [g.sync.dma_start(oa, src)], "d", ndma[0])
        out["wr"] = [(w, dur if w == i else lg) for w, lg in out["wr"]]
        ndma[0] += 1

    def store(dst, oa, ins):
        task("Y", 0.1, ins, [], lambda: [g.sync.dma_start(dst, oa)], "d", ndma[0])
        ndma[0] += 1

    def engines(a, b):
        return topo.engines(a, b)[:8]

    def send(src, sa, moves, boost=0.0):
        got, out, n = [], [], len(moves)
        trs = []
        for m, (dst, da, d) in enumerate(moves):
            to, fr = T.cores[(rank + d) % NR], T.cores[(rank - d) % NR]
            name = "r%d" % nrem[0]
            nrem[0] += 1
            rid, pid, _ = topo.addr(to)
            es = engines(core, to)
            es = es[m * len(es) // n:(m + 1) * len(es) // n]
            trs.append((rid, pid, sum(1 << e for e in es), name, da))
            got.append((name, len(engines(fr, core)) // n))
            out.append(len(es))

        def fn():
            if n == 1:
                rid, pid, mask, name, da = trs[0]
                g.remote_dma(da, sa, T.sem[name], T.sem.left, pid, rid, mask)
            else:
                g.remote_dma_fused([RemoteDMATransfer(dst_ids=[DstId(rid=rid, pnc=pid)], dma_engine_mask=mask, remote_sem=T.sem[name], src=sa, dst=da)
                                    for rid, pid, mask, name, da in trs], local_sem=T.sem.left)
            return []
        i = task("G", COST["issue"], [src], [], fn, "r", (got, sum(out)), boost)
        for m, (dst, da, d) in enumerate(moves):
            dst["wr"].append(((i, m), COST["hop"] + src["n"] * 512 / 60000.0))
        return i

    gni, nbi, thi = tile("i32", GW), tile("i32", GW), tile("i32", 1)
    XB = tile("bf", XW + L)
    X, ext = mk(XB["b"], XB["lo"], XW, True), mk(XB["b"], XB["lo"] + XW, L, True)
    a = tile("bf", L)
    load(thi, ap(thi), T.th[:], 1.8)
    gh = [mk(gni["b"], gni["lo"] + 768 * j, 768) for j in range(2)]
    for j in range(2):
        load(gh[j], ap(gh[j]), T.gn[:, 768 * j:768 * j + 768], 2.3 + 0.5 * j)
    load(nbi, ap(nbi), T.nb[:], 3.8)
    load(X, ap(X), T.x[:], 4.8)
    load(a, ap(a), T.a0[:], 4.8)
    for i in range(1, len(tasks)):
        soft(i, i - 1)

    def col(ins, src, s1, op0, s2=None, op1=None, n=1, pool="f32", f=1.0):
        t = tile(pool, n)
        ts(t, ap(t), src, s1, op0, s2, op1, ins, n, f)
        return t

    def acol(src, scale, bias):
        t = tile("f32", src["n"])
        act(t, ap(t), ap(src), AF.Identity, [src], src["n"], scale=scale, bias=bias)
        return t
    ip, ckr, ci = tile("i32", 1), tile("i32", 16), tile("i32", C)
    im, kpat = tile("f32", 144), tile("bf", 16 * CW)
    mgf, msf, ii0 = tile("f32", 128), tile("f32", 128), tile("f32", 12)
    iota(ip, [[0, 1]], 0, 1, False)
    iota(im, [[1, 144]], 0, 0)
    iota(kpat, [[0, CW], [1, 16]], 0, 0)
    iota(mgf, [[1, 8], [0, 16]], 0, 0)
    iota(ii0, [[16, 12]], 0, 0)
    iota(ckr, [[-1, 16]], 16, 1, False)
    iota(ci, [[1, C]], 0, 0, False)
    iota(msf, [[0, 8], [1, 16]], 0, 0)
    si = col([ip], ap(ip), 15, AL.bitwise_and, pool="i32")
    gi = col([ip], ap(ip), 4, AL.arith_shift_right, pool="i32")
    scol = col([si], ap(si), 0.0, AL.add)
    zc = col([gi], ap(gi), 16.0, AL.mult, 15.0, AL.add)
    gcol = col([gi], ap(gi), 0.0, AL.add)
    pcol = col([ip], ap(ip), 0.0, AL.add)
    oh0 = col([scol], ap(scol), 0.0, AL.is_equal)
    k16 = col([scol], ap(scol), 16.0, AL.add)
    rm3 = col([scol], ap(scol), 3.0, AL.is_ge)
    mask0 = col([kpat, scol], ap(kpat), ap(scol), AL.is_equal, n=16 * CW, pool="bf", f=0.5)
    Zh = col([im, zc], ap(im), ap(zc), AL.is_equal, n=144, pool="hf")
    Zb = col([im, zc], ap(im), ap(zc), AL.is_equal, n=144, pool="bf")
    Zk = col([Zh, k16], ap(Zh), ap(k16), AL.mult, n=144, pool="hf", f=0.5)
    Idb = col([im, pcol], ap(im, 0, 128), ap(pcol), AL.is_equal, n=128, pool="bf")
    Im = col([Idb], ap(Idb), -1.0, AL.mult, n=128, pool="bf", f=0.5)
    Blk = col([mgf, gcol], ap(mgf), ap(gcol), AL.is_equal, n=128, pool="bf")
    lt = col([im, pcol], ap(im, 0, 128), ap(pcol), AL.is_gt, n=128, pool="bf")
    Tri = tile("bf", 128)
    tt(Tri, ap(Tri), ap(lt), ap(Blk), AL.mult, [lt, Blk], 128, 2)
    RS = col([im, oh0], ap(im, 0, 128), 0.0, AL.mult, ap(oh0), AL.add, n=128)
    Idh = col([im, pcol], ap(im, 0, 128), ap(pcol), AL.is_equal, n=128, pool="hf")
    Lt = []
    for t in range(ST):
        eq = col([msf], ap(msf), float(t), AL.is_equal, n=128, pool="bf")
        Lt.append(tile("hf", 128))
        tt(Lt[t], ap(Lt[t]), ap(eq), ap(Blk), AL.mult, [eq, Blk], 128, 2)
    cki = col([ckr], ap(ckr), 15, AL.bitwise_and, n=16, pool="i32")
    ck = col([cki], ap(cki), 0.0, AL.add, n=16)
    cidx = tile("u16", C)
    tcopy(cidx, ap(cidx), ap(ci), [ci], C)
    ii = col([ii0, scol], ap(ii0), ap(scol), AL.add, n=12)
    hU0, I2, xi = acol(ii, 8.0, -1536.0), acol(ii, 1.0, 1536.0), acol(ii, 16.0, 0.0)
    i48, i144, one = acol(ii, 1.0, 48.0), acol(ii, -1.0, 144.0), acol(ii, 0.0, 1.0)
    ones = tile("bf", L)
    act(ones, ap(ones), ap(kpat, 0, L), AF.Identity, [kpat], L, scale=0.0, bias=1.0)
    thf = col([thi], ap(thi), 0.0, AL.add)
    own_nb = ap(nbi, 0, GW, 8)
    El0 = tile("u16", L)
    tcopy(El0, ap(El0), own_nb, [nbi], L)
    NBh0 = col([nbi], own_nb, -1536.0, AL.add, n=L)
    G = tile("f32", GW)
    for j in range(2):
        ts(G, ap(G, 768 * j, 768 * j + 768), ap(gh[j]), -1536.0, AL.add, None, None, [gh[j]], 768)
    G["mut"] = True
    NBf = tile("f32", GW)
    for j in range(4):
        ts(NBf, ap(NBf, 384 * j, 384 * j + 384), ap(nbi, 384 * j, 384 * j + 384), -1536.0, AL.add, None, None, [nbi], 384)
    own = tile("f32", 48 + L)
    act(own, ap(own, 48, 48 + L), ap(G, 0, GW, 8), AF.Copy, [G], L)

    def Z(z, k):
        return ap(z, 15 - k, 143 - k)

    lim = thf
    for gen in range(GENS):
        mo, mother = tile("hf", L), tile("hf", L)
        imo = ts(mo, ap(mo), ap(own, 48, 48 + L), ap(rm3), AL.mult, None, None, [own, rm3], L, boost=-30)
        send(mo, ap(mo), [(mother, ap(mother), 2)], boost=-30)
        hp = None
        vs, fs = [], []
        for t in range(ST):
            last = t == ST - 1
            nM = tile("hf", L)
            if t == 0:
                NBh, El, mask = NBh0, El0, mask0
                inM = ts(nM, ap(nM), ap(G, 0, GW, 8), ap(oh0), AL.mult, None, None, [G, oh0], L)
                hU, hUa, pw1 = hU0, ap(hU0), one
            else:
                PM = tile("bf", L)
                tt(PM, ap(PM), ap(hp, 0, C).indirect(ap(cidx)), ap(mask0, 0, L), AL.mult, [hp, cidx, mask0], dur=gc_(L))
                pr = ps(1)
                mms(pr, [PM, Blk], [(ap(pr, 0, L), ap(Blk), ap(PM), True, True, L)])
                prb = tile("bf", L)
                act(prb, ap(prb), ap(pr, 0, L), AF.Copy, [pr], L)
                hl = tile("u16", C)
                ts(hl, ap(hl), ap(hp, C, 2 * C), 1536.0, AL.add, None, None, [hp], C, boost=50)
                NBh, El = tile("f32", L), tile("u16", L)
                act(NBh, ap(NBh), ap(NBf).indirect(ap(hl)), AF.Copy, [NBf, hl], dur=gc_(L), boost=50)
                ts(El, ap(El), ap(NBh), 1536.0, AL.add, None, None, [NBh], L, boost=50)
                mask = ring("bf", 16 * L, "mask")
                for k in range(16 - SM, 16):
                    ab = ring("bf", L, ("ab", k))
                    act(ab, ap(ab), ap(prb), AF.Abs, [prb, ck], L, scale=-1.0, bias=ap(ck, k, k + 1))
                    act(mask, ap(mask, k, 16 * L, 16), ap(ab), AF.Relu, [ab], L, scale=-1.0, bias=1.0)
                for k in range(16 - SM):
                    ts(mask, ap(mask, k, 16 * L, 16), ap(prb), ap(ck, k, k + 1), AL.is_equal, None, None, [prb, ck], L, 0.5)
                inM = tt(nM, ap(nM), ap(G).indirect(ap(hl)), ap(mask, 0, 16 * L, 16), AL.mult, [G, hl, mask], dur=gc_(L))
                hU, hUa, pw1 = hp, ap(hp, C, 2 * C), tile("f32", C)
                act(pw1, ap(pw1), ap(hp, 0, C), AF.Identity, [hp], C, bias=1.0)
            V, Vj, iG, iW = ring("bf", 16 * L, "V"), [], [], []
            Wp = ps(0)
            for j in range(EC):
                Gg, c0, c1 = ring("hf", 16 * CW, ("Gg", j)), j * CW, j * CW + CW
                m0 = 0 if t == 0 else 16 * c0
                iG.append(tt(Gg, ap(Gg), ap(G).indirect(ap(El, c0, c1)), ap(mask, m0, m0 + 16 * CW), AL.mult, [G, El, mask], dur=gc_(16 * CW)))
                iWm = mms(Wp, [Gg, Zh], [(ap(Wp, c0, c1), Z(Zh, k), ap(Gg, k, 16 * CW, 16), k == 0, k == 15, CW) for k in range(16)])
                Wl = tile("u16", CW)
                iW.append(ts(Wl, ap(Wl), ap(Wp, c0, c1), 1536.0, AL.add, None, None, [Wp], CW, boost=50))
                Vv = mk(V["b"], V["lo"] + 16 * c0, 16 * CW, False, V["pre"])
                if VG[j] == "V":
                    tcopy(Vv, ap(Vv), ap(X).indirect(ap(Wl)), [X, Wl], dur=gc_(16 * CW))
                else:
                    act(Vv, ap(Vv), ap(X).indirect(ap(Wl)), AF.Copy, [X, Wl], dur=gc_(16 * CW))
                V["wr"] += Vv["wr"]
                Vj.append(Vv)
                if j == 0:
                    npz, dq = ps(1), ps(7)
                    mms(npz, [nM, Zh], [(ap(npz, 0, C), Z(Zh, r), ap(nM, r, L, 16), r == 0, r == 15, C) for r in range(16)])
                    nl, df = tile("u16", C), tile("bf", L)
                    inl = ts(nl, ap(nl), ap(npz, 0, C), 1536.0, AL.add, None, None, [npz], C, boost=50)
                    act(df, ap(df), ap(X).indirect(ap(nl)), AF.Copy, [X, nl], dur=gc_(L), boost=50)
                    mms(dq, [df, a, Idb, Im], [(ap(dq, 0, L), ap(Idb), ap(df), True, False, L), (ap(dq, 0, L), ap(Im), ap(a), False, True, L)], boost=50)
                    act(ext, ap(ext), ap(dq, 0, L), AF.Abs, [dq], L, boost=50)
            seq = [iG[0], inM, iW[0], iG[1], inl, iW[1], iG[2], iW[2], iG[3], iW[3]]
            if t == 0:
                soft(imo, iG[0])
            for u, v in zip(seq, seq[1:]):
                soft(v, u)
            FI, Q, ok = tile("hf", L), tile("hf", 2 * L), tile("bf", L)
            for y in range(NC):
                i0, i1 = y * W, y * W + W
                Dp = ps(2 + y)
                D = ap(Dp, 0, W)
                Te = ap(ext, i0, i1)
                vin = [Vj[j] for j in range(EC) if i0 <= j * CW < i1]
                for q in range(16 // KG):
                    Y, lst, dl = ps(4 + (y * 4 + q) % 3), [], []
                    ya = ring("bf", KG * W, ("ya", y, q))
                    for kk in range(KG):
                        k = q * KG + kk
                        o, v = ap(Y, kk * W, kk * W + W), ap(V, 16 * i0 + k, 16 * i1, 16)
                        lst += [(o, ap(Idb), v, True, False, W), (o, ap(Idb), Te, False, True, W)]
                        dl.append((D, Z(Zb, k), ap(ya, kk * W, kk * W + W), k == 0, k == 15, W))
                    mms(Y, vin + [Idb, ext], lst)
                    act(ya, ap(ya), ap(Y, 0, KG * W), AF.Abs, [Y], KG * W, bias=-255.0)
                    soft(mms(Dp, [ya, Zb], dl, after=Dp, boost=20), iWm)
                ts(ok, ap(ok, i0, i1), D, ap(lim), AL.is_le, None, None, [Dp, lim], W, boost=20)
                oky = mk(ok["b"], ok["lo"] + i0, W)
                oky["wr"] = ok["wr"][-1:]
                Cp = ps(2 + y)
                mms(Cp, [oky, Tri], [(ap(Cp, 0, W), ap(Tri), ap(oky), True, True, W)], boost=20)
                tt(FI, ap(FI, i0, i1), ap(Cp, 0, W), ap(oky), AL.is_lt, [Cp, oky], W, boost=20)
                FIy = mk(FI["b"], FI["lo"] + i0, W)
                FIy["wr"] = FI["wr"][-1:]
                tt(Q, ap(Q, i0, i1), ap(FIy), ap(NBh, i0, i1), AL.mult, [FIy, NBh], W, 2)
                tt(Q, ap(Q, L + i0, L + i1), ap(Wp, i0, i1), ap(FIy), AL.mult, [FIy, Wp], W)
            cp = ps(1)
            mms(cp, [FI, Zk], [(ap(cp, 0, C), Z(Zk, r), ap(FI, r, L, 16), r == 0, r == 15, C) for r in range(16)])
            x1, x2, nf = tile("i32", C), tile("i32", C), tile("f32", C)
            icode = tt(x1, ap(x1), ap(cp, 0, C), ap(pw1, 0, C), AL.add, [cp, pw1], C)
            ts(x2, ap(x2), ap(x1), 15, AL.bitwise_and, None, None, [x1], C)
            soft(ts(nf, ap(nf), ap(cp, 0, C), 16.0, AL.is_lt, None, None, [cp], C), icode)
            Qp, Qe = ps(7), ps(3)
            for Qx, o in ((Qp, 0), (Qe, L)):
                if Qx is Qe or not last:
                    Qs = mk(Q["b"], Q["lo"] + o, L)
                    Qs["wr"] = Q["wr"][o // L::2]
                    mms(Qx, [Qs, Zh], [(ap(Qx, 0, C), Z(Zh, r), ap(Qs, r, L, 16), r == 0, r == 15, C) for r in range(16)])
            if not last:
                Uh, ho, hp = tile("f32", C), tile("f32", 2 * C), tile("f32", 2 * C)
                tcopy(ho, ap(ho, 0, C), ap(x2), [x2], C)
                tt(Uh, ap(Uh), ap(nf), hUa, AL.mult, [nf, hU], C)
                tt(ho, ap(ho, C, 2 * C), ap(Qp, 0, C), ap(Uh), AL.add, [Qp, Uh], C)
                send(ho, ap(ho), [(hp, ap(hp), 1)])
            Ue, Re, Ll = tile("f32", C), tile("f32", C), tile("u16", C)
            tt(Ue, ap(Ue), ap(nf), ap(I2), AL.mult, [nf, I2], C)
            tt(Re, ap(Re), ap(Qe, 0, C), ap(Ue), AL.add, [Qe, Ue], C)
            iL = ts(Ll, ap(Ll), ap(Re), 1536.0, AL.add, None, None, [Re], C)
            an, a2 = tile("bf", L), tile("bf", L)
            act(an, ap(an), ap(XB).indirect(ap(Ll)), AF.Copy, [X, ext, Ll], dur=gc_(L))
            ian = send(an, ap(an), [(a2, ap(a2), 1 if not last else -2)])
            cn = ps(4)
            mms(cn, [ok, Blk], [(ap(cn, 0, L), ap(Blk), ap(ok), True, True, L)], boost=40 if last else 0)
            fl, acc, P4 = tile("bf", L), tile("f32", 1), tile("hf", L)
            act(fl, ap(fl), ap(cn, 0, L), AF.Relu, [cn], L, scale=-1.0, bias=1.0, acc=acc)
            iP4 = tt(P4, ap(P4), ap(fl), ap(nM), AL.mult, [fl, nM], L, 2)
            if not last:
                soft(iP4, iL)
                vn, vi, fi = tile("hf", L), tile("hf", L), tile("bf", L)
                tt(vn, ap(vn), ap(P4), ap(Q, L, 2 * L), AL.add, [P4, Q], L, 2)
                soft(send(fl, ap(fl), [(fi, ap(fi), 2 - t)]), ian)
                send(vn, ap(vn), [(vi, ap(vi), 2 - t)])
                vs.append([(vi, 0)])
                fs.append(fi)
            else:
                vs.append([(P4, 0), (Q, L)])
                fs.append(fl)
            pf, pl = tile("f32", C), tile("u16", C)
            tt(pf, ap(pf), ap(x2), ap(xi), AL.add, [x2, xi], C)
            tcopy(pl, ap(pl), ap(pf), [pf], C)

            def put(pl=pl, an=an):
                return [g.vector.tensor_copy(ap(X).indirect(ap(pl)), ap(an))]
            iput = task("V", gc_(L, "scatter"), [pl, an], [X], put)
            if not (gen == GENS - 1 and last):
                Ap = ps(0)
                mms(Ap, [acc, RS], [(ap(Ap, 0, 1), ap(RS), ap(acc), True, True, 1)], 4)
                A1, A2, lim = tile("i32", 1), tile("i32", 1), tile("f32", 1)
                soft(tcopy(A1, ap(A1), ap(Ap, 0, 1), [Ap], 1), iL)
                ts(A2, ap(A2), ap(A1), 63, AL.bitwise_and, None, None, [A1], 1)
                ts(lim, ap(lim), ap(A2), ap(thf), AL.add, None, None, [A2, thf], 1)
            a = a2
        Ep = ps(5)
        mms(Ep, fs + [Idb], [(ap(Ep, 0, L), ap(Idb), ap(fs[t]), t == 0, t == ST - 1, L) for t in range(ST)], boost=40)
        oh, cum = tile("bf", L), tile("bf", L)
        ts(oh, ap(oh), ap(Ep, 0, L), ap(scol), AL.is_equal, None, None, [Ep, scol], L, boost=40)

        def scan(oh=oh, cum=cum):
            return [g.vector.tensor_tensor_scan(ap(cum), ap(ones), ap(oh), 0.0, AL.mult, AL.add)]
        task("V", vc(L, 0.5), [oh, ones], [cum], scan, boost=40)
        bp = ps(5)
        mms(bp, [cum, Tri], [(ap(bp, 0, 1), ap(Tri), ap(cum, L - 1, L), True, True, 1)], boost=40)
        q1, q2 = tile("bf", L), tile("bf", L)
        tt(q1, ap(q1), ap(oh), ap(cum), AL.mult, [oh, cum], L, 2, boost=40)
        iq2 = ts(q2, ap(q2), ap(oh), ap(bp, 0, 1), AL.mult, None, None, [oh, bp], L, 0.5, boost=40)
        soft(iP4, iq2)
        soft(icode, iP4)
        op_ = ps(7)
        for q in (q1, q2):
            mms(op_, [q, Zb], [(ap(op_, 0, 12), Z(Zb, r), ap(q, r, L, 16), r == 0 and q is q1, r == 15 and q is q2, 12) for r in range(16)], boost=40, after=op_)
        po = tile("u16", 12)
        ts(po, ap(po), ap(op_, 0, 12), -1.0, AL.add, None, None, [op_], 12)
        dp, lst = ps(6), [(ap(Idh), ap(mother))]
        for t in range(ST):
            lst += [(ap(Lt[t]), ap(v, o, o + L)) for v, o in vs[t]]
        lst = [(ap(dp, 0, L), l, r, j == 0, j == len(lst) - 1, L) for j, (l, r) in enumerate(lst)]
        mms(dp, [mother, Idh] + Lt + [v for w in vs for v, _ in w], lst)
        dau, srt = tile("f32", L), tile("f32", L)
        act(dau, ap(dau), ap(dp, 0, L), AF.Copy, [dp], L)

        def scat(srt=srt, po=po, dau=dau):
            return [g.vector.tensor_copy(ap(srt).indirect(ap(po)), ap(dau))]
        y1, y2, y3, y4 = tile("f32", 12), tile("f32", 12), tile("f32", 12), tile("f32", 12)
        ts(y1, ap(y1), ap(op_, 0, 12), 145.0, AL.is_ge, None, None, [op_], 12)
        tt(y2, ap(y2), ap(i144), ap(op_, 0, 12), AL.subtract, [i144, op_], 12)
        tt(y3, ap(y3), ap(y1), ap(y2), AL.mult, [y1, y2], 12)
        iy4 = tt(y4, ap(y4), ap(y3), ap(i48), AL.add, [y3, i48], 12)
        Lm, Ln, prev = tile("f32", 12), tile("u16", 12), tile("f32", 48)
        send(y4, ap(y4), [(Lm, ap(Lm), -2)])
        isc = task("V", gc_(L, "scatter"), [po, dau], [srt], scat)
        soft(isc, iy4)
        soft(iput, isc)
        best = mk(srt["b"], srt["lo"], 48)
        best["wr"] = srt["wr"]
        soft(ian, send(best, ap(best), [(own, ap(own, 0, 48), -2), (prev, ap(prev), -1)]))
        tcopy(Ln, ap(Ln), ap(Lm), [Lm], 12)
        own2 = mk(own["b"], own["lo"], own["n"])
        own2["wr"] = list(own["wr"])
        tcopy(own2, ap(own, 1, 48, 2), ap(prev, 1, 48, 2), [own, prev], 24)
        new = tile("f32", 48 + L)
        tcopy(new, ap(new, 48, 48 + L), ap(own).indirect(ap(Ln)), [own2, Ln], dur=gc_(L))
        if gen < GENS - 1:
            tcopy(G, ap(G, 0, GW, 8), ap(new, 48, 48 + L), [new], L)
        own = new
    yo, ao, so = tile("f32", L), tile("f32", L), tile("f32", L)
    act(yo, ap(yo), ap(own, 48, 48 + L), AF.Copy, [own], L, bias=1536.0)
    store(T.yg[:], ap(yo), [yo])
    act(ao, ap(ao), ap(a), AF.Copy, [a], L)
    store(T.ya[:], ap(ao), [ao])
    sp = ps(0)
    mms(sp, [X, Idb], [(ap(sp, 0, L), ap(Idb), ap(X, s, XW, 16), s == 0, s == 15, L) for s in range(16)])
    act(so, ap(so), ap(sp, 0, L), AF.Copy, [sp], L)
    store(T.ys[:], ap(so), [so])
    emit(g, T, tasks)


def tid(d):
    return d[0] if isinstance(d, tuple) else d


def order(tasks):
    n = len(tasks)
    succ, left = [[] for _ in range(n)], [0] * n
    for i, t in enumerate(tasks):
        for d, lag in t["deps"].items():
            succ[tid(d)].append((i, lag))
        left[i] = len(t["deps"])
    need, topo_order = list(left), [i for i in range(n) if not left[i]]
    for i in topo_order:
        for j, _ in succ[i]:
            need[j] -= 1
            if not need[j]:
                topo_order.append(j)
    assert len(topo_order) == n
    prio = [0.0] * n
    for i in reversed(topo_order):
        prio[i] = tasks[i]["dur"] + max([prio[j] + COST["sem"] + lag for j, lag in succ[i]], default=0.0)
    free, fin, out = {}, [0.0] * n, []
    avail = {i: 0.0 for i in range(n) if not left[i]}
    while avail:
        st, _, i = min((max(r, free.get(tasks[i]["q"], 0.0)), -prio[i] - tasks[i]["boost"], i) for i, r in avail.items())
        del avail[i]
        fin[i] = free[tasks[i]["q"]] = st + tasks[i]["dur"]
        out.append(i)
        for j, _ in succ[i]:
            left[j] -= 1
            if not left[j]:
                avail[j] = max(fin[tid(d)] + lag + COST["sem"] for d, lag in tasks[j]["deps"].items())
    return out


def emit(g, T, tasks):
    eng = {"V": g.vector, "S": g.scalar, "P": g.tensor, "G": g, "Y": g.sync}
    sem_of = {"V": "sV", "S": "sS", "P": "sP", "G": "sG"}
    count = {s: 0 for s in sem_of.values()}
    known, done = {q: {} for q in eng}, {}
    sent, ends = 0, []
    for i in order(tasks):
        t = tasks[i]
        q = t["q"]
        k, need = known[q], {}
        for d in t["deps"]:
            if d in t["soft"]:
                continue
            s, v, kn = done[d]
            if k.get(s, 0) < v and need.get(s, (0, None))[0] < v:
                need[s] = (v, kn)
        for s in sorted(need, key=lambda s: -len(need[s][1])):
            v, kn = need[s]
            if k.get(s, 0) >= v or any(o != s and need[o][1].get(s, 0) >= v and k.get(o, 0) < need[o][0] for o in need):
                continue
            eng[q].wait_ge(T.sem[s], v)
            for b, w in kn.items():
                k[b] = max(k.get(b, 0), w)
            k[s] = max(v, k.get(s, 0))
        for s, (v, kn) in need.items():
            if k.get(s, 0) < v:
                eng[q].wait_ge(T.sem[s], v)
                k[s] = v
        ins = t["fn"]()
        if t["kind"] == "c":
            s = sem_of[q]
            for m in ins:
                m.then_inc(T.sem[s], 1)
            count[s] += len(ins)
            done[i] = (s, count[s], dict(k))
        elif t["kind"] == "d":
            s = "d%d" % t["x"]
            ins[0].then_inc(T.sem[s], 16)
            done[i] = (s, 16, dict(k))
            ends.append((s, 16))
        else:
            got, out = t["x"]
            sent += out
            for m, (name, c) in enumerate(got):
                done[(i, m)] = (name, c, {})
                ends.append((name, c))
    for s, v in ends + [("left", sent)] + list(count.items()):
        if known["Y"].get(s, 0) < v:
            g.sync.wait_ge(T.sem[s], v)
